import numpy as np
import ml_dtypes


def mxq(x, axis, fmt="e4m3"):
    dtype, down = {"e4m3": (ml_dtypes.float8_e4m3fn, 7), "e5m2": (ml_dtypes.float8_e5m2, 14)}[fmt]
    v = np.moveaxis(np.asarray(x, np.float32).astype(ml_dtypes.bfloat16).astype(np.float64), axis, -1)
    blocks = v.reshape(v.shape[:-1] + (-1, 32))
    amax = np.abs(blocks).max(-1, keepdims=True)
    byte = np.maximum(np.where(amax > 0, np.frexp(amax)[1] - 1 + 127, 0) - down, 1)
    scale = np.exp2(byte - 127.0)
    codes = (blocks / scale).astype(np.float32).astype(dtype).astype(np.float64)
    return np.moveaxis((codes * scale).reshape(v.shape), -1, axis)


WIDE = False


def mx_kscale(k):
    if not WIDE:
        return np.ones(k)
    levels = np.array([10, -10, 5, -5, 0])
    if k % 512:
        return np.exp2(np.random.permutation(np.resize(levels, k // 32))).repeat(32)
    a = np.empty((k // 512, 16))
    for p in range(k // 512):
        a[p, :8] = np.random.permutation(np.resize(levels, 8))
        for g in range(8):
            far = levels[np.abs(levels - a[p, g]) >= 10]
            a[p, g + 8] = far[np.random.randint(len(far))]
    return np.exp2(a.ravel()).repeat(32)


def f64(x):
    return np.asarray(x).astype(np.float64)


def striped(idx):
    return np.tile(idx.reshape(-1, 16).T, (8, 1)).astype(np.uint16)


def unstriped(offs):
    return offs[:16].T.reshape(-1).astype(np.int64)


E2M1 = np.array([0.0, 0.5, 1.0, 1.5, 2.0, 3.0, 4.0, 6.0, -0.0, -0.5, -1.0, -1.5, -2.0, -3.0, -4.0, -6.0])


def pack_weight(w, fmt):
    k, n = w.shape
    w = f64(np.asarray(w, np.float32).astype(ml_dtypes.bfloat16)).reshape(k // 32, 32, n)
    amax = np.abs(w).max(1)
    if fmt == "e4m3":
        byte = np.frexp(amax)[1] - 1 + 127 - 7
    else:
        mant, ex = np.frexp(amax / 6.0)
        byte = np.where(mant > 0.5, ex, ex - 1) + 127
    byte = np.clip(np.where(amax > 0, byte, 1), 1, 254)
    scaled = (w * np.exp2(127.0 - byte)[:, None, :]).reshape(k, n).astype(np.float32)
    by_word = np.ascontiguousarray(scaled.reshape(k // 512, 128, 4, n).transpose(0, 1, 3, 2))
    if fmt == "e4m3":
        words = by_word.astype(ml_dtypes.float8_e4m3fn).view(np.uint8)
    else:
        c = by_word.astype(ml_dtypes.float4_e2m1fn).view(np.uint8) & 0xF
        words = (c[..., 0::2] | (c[..., 1::2] << 4)).reshape(k // 512, 128, 2 * n)
    return np.ascontiguousarray(words), np.ascontiguousarray(byte.astype(np.uint8).reshape(k // 512, 16, n))


def unpack_weight(words, scales, fmt):
    g, _, n = scales.shape
    words = np.ascontiguousarray(words).reshape(g, 128, n, -1)
    if fmt == "e4m3":
        vals = words.view(ml_dtypes.float8_e4m3fn).astype(np.float64)
    else:
        nib = np.empty((g, 128, n, 4), np.uint8)
        nib[..., 0::2] = words & 0xF
        nib[..., 1::2] = words >> 4
        vals = E2M1[nib]
    vals = vals * np.repeat(np.exp2(scales.astype(np.float64) - 127.0), 8, axis=1)[..., None]
    return vals.transpose(0, 1, 3, 2).reshape(g * 512, n)


def sigmoid(v):
    return 1.0 / (1.0 + np.exp(-np.maximum(v, -700.0)))


K, T, E, C, H, N, HOT = 1536, 768, 6, 128, 512, 128, 1


def by_expert(wq, xq):
    return np.concatenate([wq[e].T @ xq[:, e * C:(e + 1) * C] for e in range(E)], axis=1)


def setup_inputs():
    n = np.random.standard_normal
    s = mx_kscale(K)
    u = mx_kscale(H)
    slot_token = np.concatenate([np.random.permutation(T)[:C] for e in range(E)])
    x = pack_weight(n((K, T)) * s[:, None], "e4m3")
    w1h = [pack_weight(m, "e4m3") for m in n((HOT, K, H)) / np.sqrt(K) / s[None, :, None]]
    w3h = [pack_weight(m, "e4m3") for m in n((HOT, K, H)) / np.sqrt(K) / s[None, :, None] * u]
    w2h = [pack_weight(m, "e4m3") for m in n((HOT, H, N)) / np.sqrt(H) / u[None, :, None]]
    w1c = [pack_weight(m, "e2m1") for m in n((E - HOT, K, H)) / np.sqrt(K) / s[None, :, None]]
    w3c = [pack_weight(m, "e2m1") for m in n((E - HOT, K, H)) / np.sqrt(K) / s[None, :, None] * u]
    w2c = [pack_weight(m, "e2m1") for m in n((E - HOT, H, N)) / np.sqrt(H) / u[None, :, None]]
    return {
        "x_words": x[0],
        "x_scales": x[1],
        "w1h_words": np.stack([m[0] for m in w1h]),
        "w1h_scales": np.stack([m[1] for m in w1h]),
        "w3h_words": np.stack([m[0] for m in w3h]),
        "w3h_scales": np.stack([m[1] for m in w3h]),
        "w2h_words": np.stack([m[0] for m in w2h]),
        "w2h_scales": np.stack([m[1] for m in w2h]),
        "w1c_words": np.stack([m[0] for m in w1c]),
        "w1c_scales": np.stack([m[1] for m in w1c]),
        "w3c_words": np.stack([m[0] for m in w3c]),
        "w3c_scales": np.stack([m[1] for m in w3c]),
        "w2c_words": np.stack([m[0] for m in w2c]),
        "w2c_scales": np.stack([m[1] for m in w2c]),
        "offs": striped(slot_token),
    }


def reference(x_words, x_scales, w1h_words, w1h_scales, w3h_words, w3h_scales, w2h_words, w2h_scales, w1c_words, w1c_scales, w3c_words, w3c_scales, w2c_words, w2c_scales, offs):
    w1h = np.stack([unpack_weight(w1h_words[e], w1h_scales[e], "e4m3") for e in range(HOT)])
    w3h = np.stack([unpack_weight(w3h_words[e], w3h_scales[e], "e4m3") for e in range(HOT)])
    w2h = np.stack([unpack_weight(w2h_words[e], w2h_scales[e], "e4m3") for e in range(HOT)])
    w1c = np.stack([unpack_weight(w1c_words[e], w1c_scales[e], "e2m1") for e in range(E - HOT)])
    w3c = np.stack([unpack_weight(w3c_words[e], w3c_scales[e], "e2m1") for e in range(E - HOT)])
    w2c = np.stack([unpack_weight(w2c_words[e], w2c_scales[e], "e2m1") for e in range(E - HOT)])
    idx = unstriped(offs)
    xq = unpack_weight(x_words, x_scales, "e4m3")[:, idx]
    w1 = [*w1h, *w1c]
    w3 = [*w3h, *w3c]
    w2 = [*w2h, *w2c]
    h = sigmoid(by_expert(w1, xq)) * by_expert(w3, xq)
    y = by_expert(w2, mxq(h, 0, "e4m3"))
    out = y
    return out

@@ -1,0 +1,199 @@
+from contextlib import ExitStack
+
+import concourse.mybir as mybir
+from concourse.masks import make_identity
+
+K, T, E, C, H, N = 1536, 768, 6, 128, 512, 128
+P = 128
+PASSES = K // 512
+COLD = E - 1
+FLOPS = 2 * E * C * (2 * K * H + H * N)
+
+F32 = mybir.dt.float32
+BF16 = mybir.dt.bfloat16
+I32 = mybir.dt.int32
+U32 = mybir.dt.uint32
+U16 = mybir.dt.uint16
+U8 = mybir.dt.uint8
+FP8X4 = mybir.dt.float8_e4m3fn_x4
+FP4X4 = mybir.dt.float4_e2m1fn_x4
+SIGMOID = mybir.ActivationFunctionType.Sigmoid
+MULT = mybir.AluOpType.mult
+
+ORDER = [1, 2, 3, 4, 5, 0]
+GROUPS = [(1, 4), (4, 6), (0, 1)]
+GATHERS = [(1, 2), (2, 4), (4, 6)]
+
+
+def tile_moe_hot_s_glu_sigmoid_kernel(
+    tc, x_words, x_scales, w1h_words, w1h_scales, w3h_words, w3h_scales, w2h_words, w2h_scales,
+    w1c_words, w1c_scales, w3c_words, w3c_scales, w2c_words, w2c_scales, offs, out,
+):
+    nc = tc.nc
+    with ExitStack() as ctx:
+        held = ctx.enter_context(tc.tile_pool(name="held", bufs=1))
+        ring = ctx.enter_context(tc.tile_pool(name="ring", bufs=3))
+        psum = ctx.enter_context(tc.psum_pool(name="psum", bufs=1))
+
+        offsets = held.tile([P, E * C // 16], U16, name="offsets")
+        nc.sync.dma_start(offsets[:], offs)
+
+        def plane(name, rows, width, engine=nc.vector):
+            t = held.tile([P, rows, width], U8, name=name, align_bytes=64)
+            engine.memset(t[:].rearrange("p a n -> p (a n)").bitcast(I32), 0)
+            return t
+
+        xs = plane("xs", PASSES, T, nc.gpsimd)
+        s1c = plane("s1c", COLD * PASSES, H)
+        s3c = plane("s3c", COLD * PASSES, H)
+        s2c = plane("s2c", COLD, N)
+        s2h = plane("s2h", 1, N)
+        s1h = plane("s1h", PASSES, H)
+        s3h = plane("s3h", PASSES, H)
+
+        def load_rows(t, src, r, queue=nc.sync):
+            rows = src.rearrange("a (q r) n -> r q a n", r=4)[r]
+            queue.dma_start(t[:].bitcast(I32)[r:P:32, :, :], rows)
+
+        def flat(scales):
+            return scales.bitcast(I32).rearrange("f s b n -> (f s) b n")
+
+        xw = [held.tile([P, T], I32, name="xw%d" % s, align_bytes=64) for s in range(PASSES)]
+        for s in range(PASSES):
+            nc.sync.dma_start(xw[s][:], x_words[s].rearrange("p t d -> p (t d)").bitcast(I32))
+        for r in range(4):
+            load_rows(xs, x_scales.bitcast(I32), r, nc.scalar)
+        for t, src in ((s1c, w1c_scales), (s3c, w3c_scales), (s2c, w2c_scales)):
+            for r in range(4):
+                load_rows(t, flat(src), r)
+        late = [(t, flat(src), r) for t, src in ((s2h, w2h_scales), (s1h, w1h_scales), (s3h, w3h_scales)) for r in range(4)]
+
+        w1 = {}
+        w3 = {}
+        for i, e in enumerate(ORDER[:-1]):
+            w1[e] = held.tile([P, PASSES, 2 * H], U8, name="w1_%d" % e, align_bytes=64)
+            w3[e] = held.tile([P, PASSES, 2 * H], U8, name="w3_%d" % e, align_bytes=64)
+            nc.sync.dma_start(w1[e][:].bitcast(I32), w1c_words[e - 1].rearrange("s p n -> p s n").bitcast(I32))
+            nc.sync.dma_start(w3[e][:].bitcast(I32), w3c_words[e - 1].rearrange("s p n -> p s n").bitcast(I32))
+            if i == 0:
+                w2c = held.tile([P, COLD, 2 * N], U8, name="w2c", align_bytes=64)
+                nc.sync.dma_start(w2c[:].bitcast(I32), w2c_words.bitcast(I32).rearrange("f s p n -> p (f s) n"))
+                w2h = held.tile([P, 4 * N], U8, name="w2h", align_bytes=64)
+                nc.sync.dma_start(w2h[:].bitcast(I32), w2h_words[0, 0].rearrange("p n d -> p (n d)").bitcast(I32))
+            else:
+                for item in late[3 * (i - 1) : 3 * i]:
+                    load_rows(*item)
+        w1[0] = held.tile([P, PASSES, 4 * H], U8, name="w1_0", align_bytes=64)
+        w3[0] = held.tile([P, PASSES, 4 * H], U8, name="w3_0", align_bytes=64)
+        nc.sync.dma_start(w1[0][:].bitcast(I32), w1h_words[0].rearrange("s p n d -> p s (n d)").bitcast(I32))
+        for s in range(PASSES):
+            nc.sync.dma_start(w3[0][:, s, :].bitcast(I32), w3h_words[0, s].rearrange("p n d -> p (n d)").bitcast(I32))
+
+        ident = held.tile([P, P], F32, name="ident")
+        make_identity(nc, ident[:])
+        warm = held.tile([P, 1], F32, name="warm")
+        nc.scalar.activation(warm[:], ident[:, 0:1], SIGMOID)
+
+        gw = held.tile([P, PASSES, COLD * C], U32, name="gw", align_bytes=64)
+        gs = held.tile([P, PASSES, COLD * C], U8, name="gs", align_bytes=64)
+
+        def columns(first, end, s):
+            place = first - 1 if first else s
+            return slice(place * C, (place + end - first) * C)
+
+        def gather(first, end, s):
+            entries = offsets[:, first * C // 16 : end * C // 16]
+            nc.vector.tensor_copy(gw[:, s, columns(first, end, s)], xw[s][:].bitcast(U32).indirect(entries))
+            nc.vector.tensor_copy(gs[:, s, columns(first, end, s)], xs[:, s, :].indirect(entries))
+
+        for first, end in GATHERS:
+            for s in range(PASSES):
+                gather(first, end, s)
+
+        ysb = held.tile([P, E * C], F32, name="ysb")
+
+        def first_layer(e, words, cold_plane, hot_plane, acc):
+            for s in range(PASSES):
+                slots = columns(e, e + 1, s)
+                nc.tensor.matmul_mx(
+                    out=acc[:],
+                    lhsT=gw[:, s, slots].bitcast(FP8X4),
+                    lhsT_scale=gs[:, s, slots],
+                    rhs=words[:, s, :].bitcast(FP4X4 if e else FP8X4),
+                    rhs_scale=cold_plane[:, (e - 1) * PASSES + s, :] if e else hot_plane[:, s, :],
+                    start=(s == 0),
+                    stop=(s == PASSES - 1),
+                )
+
+        gate_banks = [psum.tile([P, H], F32, name="gate_bank%d" % j) for j in range(3)]
+        lin_banks = [psum.tile([P, H], F32, name="lin_bank%d" % j) for j in range(3)]
+        spare = [psum.tile([P, H], F32, name="spare%d" % j) for j in range(2)]
+
+        def turned_in(i):
+            bank = gate_banks[(i + 1) % 3] if i + 1 < E else spare[0]
+            return bank[:, 0 : 2 * C]
+
+        def result_in(i):
+            bank = gate_banks[(i + 2) % 3] if i + 2 < E else spare[(i + 1) % 2]
+            return bank[:, 2 * C : 3 * C]
+
+        def hidden(i):
+            e = ORDER[i]
+            a, b = gate_banks[i % 3], lin_banks[i % 3]
+            first_layer(e, w1[e], s1c, s1h, a)
+            first_layer(e, w3[e], s3c, s3h, b)
+            gate = ring.tile([P, 2, P, 2], F32, name="gate")
+            nc.scalar.activation(gate[:], a[:].rearrange("j (p u v) -> j u p v", u=2, v=2), SIGMOID)
+            h = ring.tile([P, 2, P, 2], BF16, name="h", align_bytes=64)
+            nc.vector.tensor_tensor(h[:], b[:].rearrange("j (p u v) -> j u p v", u=2, v=2), gate[:], MULT)
+            return h
+
+        def turn(i, h):
+            pairs = h[:].rearrange("j u p v -> j (u p v)").bitcast(F32)
+            for u in range(2):
+                nc.tensor.transpose(turned_in(i)[:, u * C : (u + 1) * C], pairs[:, u * P : (u + 1) * P], ident[:])
+
+        def quantise(i):
+            ht = ring.tile([P, 4 * C], BF16, name="ht", align_bytes=64)
+            nc.scalar.copy(
+                ht[:].bitcast(F32).rearrange("p (j u) -> p j u", u=2),
+                turned_in(i).rearrange("p (u j) -> p j u", u=2),
+            )
+            codes = ring.tile([P, C], U32, name="codes", align_bytes=64)
+            scales = ring.tile([P, C], U8, name="scales", align_bytes=64)
+            nc.vector.quantize_mx(out=codes[:].bitcast(FP8X4), scales=scales[:], in_=ht[:])
+            return codes, scales
+
+        def second_layer(i, codes, scales):
+            e = ORDER[i]
+            nc.tensor.matmul_mx(
+                out=result_in(i),
+                lhsT=w2c[:, e - 1, :].bitcast(FP4X4) if e else w2h[:].bitcast(FP8X4),
+                lhsT_scale=s2c[:, e - 1, :] if e else s2h[:, 0, :],
+                rhs=codes[:].bitcast(FP8X4),
+                rhs_scale=scales[:],
+                start=True,
+                stop=True,
+            )
+
+        def store(i):
+            e = ORDER[i]
+            nc.scalar.copy(ysb[:, e * C : (e + 1) * C], result_in(i))
+            for first, end in GROUPS:
+                if e == end - 1:
+                    nc.sync.dma_start(out[:, first * C : end * C], ysb[:, first * C : end * C])
+
+        hs = {}
+        quantised = {}
+        for i in range(E + 2):
+            if i < E:
+                hs[i] = hidden(i)
+            if i >= 2:
+                second_layer(i - 2, *quantised[i - 2])
+            if 1 <= i <= E:
+                turn(i - 1, hs[i - 1])
+                quantised[i - 1] = quantise(i - 1)
+            if i >= 2:
+                store(i - 2)
+            if i < PASSES:
+                gather(0, 1, i)

@@ -22,7 +22,9 @@ MULT = mybir.AluOpType.mult
 
 ORDER = [1, 2, 3, 4, 5, 0]
 GROUPS = [(1, 4), (4, 6), (0, 1)]
-GATHERS = [(1, 2), (2, 4), (4, 6)]
+GATHERS = [(1, 2), (2, 4)]
+SCALE_GROUPS = [(1, 3), (3, 6)]
+AHEAD = 3
 
 
 def tile_moe_hot_s_glu_sigmoid_kernel(
@@ -44,9 +46,13 @@ def tile_moe_hot_s_glu_sigmoid_kernel(
             return t
 
         xs = plane("xs", PASSES, T, nc.gpsimd)
-        s1c = plane("s1c", COLD * PASSES, H)
-        s3c = plane("s3c", COLD * PASSES, H)
-        s2c = plane("s2c", COLD, N)
+        s1c = {}
+        s3c = {}
+        for first, end in SCALE_GROUPS:
+            s1c[first] = plane("s1c%d" % first, (end - first) * PASSES, H)
+            s3c[first] = plane("s3c%d" % first, (end - first) * PASSES, H)
+            if first == ORDER[0]:
+                s2c = plane("s2c", COLD, N)
         s2h = plane("s2h", 1, N)
         s1h = plane("s1h", PASSES, H)
         s3h = plane("s3h", PASSES, H)
@@ -63,42 +69,46 @@ def tile_moe_hot_s_glu_sigmoid_kernel(
             nc.sync.dma_start(xw[s][:], x_words[s].rearrange("p t d -> p (t d)").bitcast(I32))
         for r in range(4):
             load_rows(xs, x_scales.bitcast(I32), r, nc.scalar)
-        for t, src in ((s1c, w1c_scales), (s3c, w3c_scales), (s2c, w2c_scales)):
-            for r in range(4):
-                load_rows(t, flat(src), r)
-        late = [(t, flat(src), r) for t, src in ((s2h, w2h_scales), (s1h, w1h_scales), (s3h, w3h_scales)) for r in range(4)]
+        late = [(t, flat(src), r) for t, src in ((s1h, w1h_scales), (s3h, w3h_scales)) for r in range(4)]
 
         w1 = {}
         w3 = {}
         for i, e in enumerate(ORDER[:-1]):
+            for first, end in SCALE_GROUPS:
+                if e == first:
+                    for t, src in ((s1c, w1c_scales), (s3c, w3c_scales)):
+                        for r in range(4):
+                            load_rows(t[e], flat(src[first - 1 : end - 1]), r)
             w1[e] = held.tile([P, PASSES, 2 * H], U8, name="w1_%d" % e, align_bytes=64)
             w3[e] = held.tile([P, PASSES, 2 * H], U8, name="w3_%d" % e, align_bytes=64)
             nc.sync.dma_start(w1[e][:].bitcast(I32), w1c_words[e - 1].rearrange("s p n -> p s n").bitcast(I32))
             nc.sync.dma_start(w3[e][:].bitcast(I32), w3c_words[e - 1].rearrange("s p n -> p s n").bitcast(I32))
-            if i == 0:
+            if i == 1:
+                for r in range(4):
+                    load_rows(s2c, flat(w2c_scales), r)
                 w2c = held.tile([P, COLD, 2 * N], U8, name="w2c", align_bytes=64)
                 nc.sync.dma_start(w2c[:].bitcast(I32), w2c_words.bitcast(I32).rearrange("f s p n -> p (f s) n"))
-                w2h = held.tile([P, 4 * N], U8, name="w2h", align_bytes=64)
-                nc.sync.dma_start(w2h[:].bitcast(I32), w2h_words[0, 0].rearrange("p n d -> p (n d)").bitcast(I32))
-            else:
-                for item in late[3 * (i - 1) : 3 * i]:
+            if i >= 2:
+                for item in late[3 * (i - 2) : 3 * (i - 1)]:
                     load_rows(*item)
         w1[0] = held.tile([P, PASSES, 4 * H], U8, name="w1_0", align_bytes=64)
         w3[0] = held.tile([P, PASSES, 4 * H], U8, name="w3_0", align_bytes=64)
         nc.sync.dma_start(w1[0][:].bitcast(I32), w1h_words[0].rearrange("s p n d -> p s (n d)").bitcast(I32))
         for s in range(PASSES):
             nc.sync.dma_start(w3[0][:, s, :].bitcast(I32), w3h_words[0, s].rearrange("p n d -> p (n d)").bitcast(I32))
+        w2h = held.tile([P, 4 * N], U8, name="w2h", align_bytes=64)
+        nc.sync.dma_start(w2h[:].bitcast(I32), w2h_words[0, 0].rearrange("p n d -> p (n d)").bitcast(I32))
+        for r in range(4):
+            load_rows(s2h, flat(w2h_scales), r)
 
         ident = held.tile([P, P], F32, name="ident")
         make_identity(nc, ident[:])
-        warm = held.tile([P, 1], F32, name="warm")
-        nc.scalar.activation(warm[:], ident[:, 0:1], SIGMOID)
 
-        gw = held.tile([P, PASSES, COLD * C], U32, name="gw", align_bytes=64)
-        gs = held.tile([P, PASSES, COLD * C], U8, name="gs", align_bytes=64)
+        gw = held.tile([P, PASSES, AHEAD * C], U32, name="gw", align_bytes=64)
+        gs = held.tile([P, PASSES, AHEAD * C], U8, name="gs", align_bytes=64)
 
         def columns(first, end, s):
-            place = first - 1 if first else s
+            place = ORDER.index(first) % AHEAD
             return slice(place * C, (place + end - first) * C)
 
         def gather(first, end, s):
@@ -112,6 +122,10 @@ def tile_moe_hot_s_glu_sigmoid_kernel(
 
         ysb = held.tile([P, E * C], F32, name="ysb")
 
+        def cold_rows(planes, e, s):
+            first = max(f for f in planes if f <= e)
+            return planes[first][:, (e - first) * PASSES + s, :]
+
         def first_layer(e, words, cold_plane, hot_plane, acc):
             for s in range(PASSES):
                 slots = columns(e, e + 1, s)
@@ -120,7 +134,7 @@ def tile_moe_hot_s_glu_sigmoid_kernel(
                     lhsT=gw[:, s, slots].bitcast(FP8X4),
                     lhsT_scale=gs[:, s, slots],
                     rhs=words[:, s, :].bitcast(FP4X4 if e else FP8X4),
-                    rhs_scale=cold_plane[:, (e - 1) * PASSES + s, :] if e else hot_plane[:, s, :],
+                    rhs_scale=cold_rows(cold_plane, e, s) if e else hot_plane[:, s, :],
                     start=(s == 0),
                     stop=(s == PASSES - 1),
                 )
@@ -195,5 +209,6 @@ def tile_moe_hot_s_glu_sigmoid_kernel(
                 quantised[i - 1] = quantise(i - 1)
             if i >= 2:
                 store(i - 2)
-            if i < PASSES:
-                gather(0, 1, i)
+            if i + AHEAD < E:
+                for s in range(PASSES):
+                    gather(ORDER[i + AHEAD], ORDER[i + AHEAD] + 1, s)

@@ -23,7 +23,7 @@ MULT = mybir.AluOpType.mult
 ORDER = [1, 2, 3, 4, 5, 0]
 GROUPS = [(1, 4), (4, 6), (0, 1)]
 GATHERS = [(1, 2), (2, 4)]
-SCALE_GROUPS = [(1, 3), (3, 6)]
+SCALE_GROUPS = [(1, 4), (4, 6)]
 AHEAD = 3
 
 
@@ -88,8 +88,8 @@ def tile_moe_hot_s_glu_sigmoid_kernel(
                     load_rows(s2c, flat(w2c_scales), r)
                 w2c = held.tile([P, COLD, 2 * N], U8, name="w2c", align_bytes=64)
                 nc.sync.dma_start(w2c[:].bitcast(I32), w2c_words.bitcast(I32).rearrange("f s p n -> p (f s) n"))
-            if i >= 2:
-                for item in late[3 * (i - 2) : 3 * (i - 1)]:
+            if i >= 3:
+                for item in late[4 * (i - 3) : 4 * (i - 2)]:
                     load_rows(*item)
         w1[0] = held.tile([P, PASSES, 4 * H], U8, name="w1_0", align_bytes=64)
         w3[0] = held.tile([P, PASSES, 4 * H], U8, name="w3_0", align_bytes=64)

@@ -21,7 +21,7 @@ SIGMOID = mybir.ActivationFunctionType.Sigmoid
 MULT = mybir.AluOpType.mult
 
 ORDER = [1, 2, 3, 4, 5, 0]
-GROUPS = [(1, 4), (4, 6), (0, 1)]
+EARLY = 2
 GATHERS = [(1, 2), (2, 4)]
 SCALE_GROUPS = [(1, 4), (4, 6)]
 AHEAD = 3
@@ -71,6 +71,11 @@ def tile_moe_hot_s_glu_sigmoid_kernel(
             load_rows(xs, x_scales.bitcast(I32), r, nc.scalar)
         late = [(t, flat(src), r) for t, src in ((s1h, w1h_scales), (s3h, w3h_scales)) for r in range(4)]
 
+        def load_second(first, end):
+            t = held.tile([P, end - first, 2 * N], U8, name="w2c%d" % first, align_bytes=64)
+            nc.sync.dma_start(t[:].bitcast(I32), w2c_words[first - 1 : end - 1].bitcast(I32).rearrange("f s p n -> p (f s) n"))
+            return {e: t[:, e - first, :].bitcast(FP4X4) for e in range(first, end)}
+
         w1 = {}
         w3 = {}
         for i, e in enumerate(ORDER[:-1]):
@@ -86,16 +91,21 @@ def tile_moe_hot_s_glu_sigmoid_kernel(
             if i == 1:
                 for r in range(4):
                     load_rows(s2c, flat(w2c_scales), r)
-                w2c = held.tile([P, COLD, 2 * N], U8, name="w2c", align_bytes=64)
-                nc.sync.dma_start(w2c[:].bitcast(I32), w2c_words.bitcast(I32).rearrange("f s p n -> p (f s) n"))
+                w2 = load_second(1, EARLY + 1)
             if i >= 3:
                 for item in late[4 * (i - 3) : 4 * (i - 2)]:
                     load_rows(*item)
         w1[0] = held.tile([P, PASSES, 4 * H], U8, name="w1_0", align_bytes=64)
-        w3[0] = held.tile([P, PASSES, 4 * H], U8, name="w3_0", align_bytes=64)
         nc.sync.dma_start(w1[0][:].bitcast(I32), w1h_words[0].rearrange("s p n d -> p s (n d)").bitcast(I32))
+        hot3 = {}
         for s in range(PASSES):
-            nc.sync.dma_start(w3[0][:, s, :].bitcast(I32), w3h_words[0, s].rearrange("p n d -> p (n d)").bitcast(I32))
+            src = w3h_words[0, s].rearrange("p n d -> p (n d)").bitcast(I32)
+            for first, end in [(0, 2)] if s < PASSES - 1 else [(0, 1), (1, 2)]:
+                t = held.tile([P, (end - first) * 2 * H], U8, name="w3h_%d_%d" % (s, first), align_bytes=64)
+                nc.sync.dma_start(t[:].bitcast(I32), src[:, first * H // 2 : end * H // 2])
+                for u in range(first, end):
+                    hot3[(s, u)] = t[:, (u - first) * 2 * H : (u - first + 1) * 2 * H]
+        w2.update(load_second(EARLY + 1, E))
         w2h = held.tile([P, 4 * N], U8, name="w2h", align_bytes=64)
         nc.sync.dma_start(w2h[:].bitcast(I32), w2h_words[0, 0].rearrange("p n d -> p (n d)").bitcast(I32))
         for r in range(4):
@@ -126,18 +136,21 @@ def tile_moe_hot_s_glu_sigmoid_kernel(
             first = max(f for f in planes if f <= e)
             return planes[first][:, (e - first) * PASSES + s, :]
 
-        def first_layer(e, words, cold_plane, hot_plane, acc):
+        def first_layer(e, words, scales, acc):
             for s in range(PASSES):
                 slots = columns(e, e + 1, s)
                 nc.tensor.matmul_mx(
-                    out=acc[:],
+                    out=acc,
                     lhsT=gw[:, s, slots].bitcast(FP8X4),
                     lhsT_scale=gs[:, s, slots],
-                    rhs=words[:, s, :].bitcast(FP4X4 if e else FP8X4),
-                    rhs_scale=cold_rows(cold_plane, e, s) if e else hot_plane[:, s, :],
+                    rhs=words[s].bitcast(FP4X4 if e else FP8X4),
+                    rhs_scale=scales[s],
                     start=(s == 0),
                     stop=(s == PASSES - 1),
                 )
+
+        def paired(acc):
+            return acc.rearrange("j (p u v) -> j u p v", u=2, v=2)
 
         gate_banks = [psum.tile([P, H], F32, name="gate_bank%d" % j) for j in range(3)]
         lin_banks = [psum.tile([P, H], F32, name="lin_bank%d" % j) for j in range(3)]
@@ -148,18 +161,28 @@ def tile_moe_hot_s_glu_sigmoid_kernel(
             return bank[:, 0 : 2 * C]
 
         def result_in(i):
-            bank = gate_banks[(i + 2) % 3] if i + 2 < E else spare[(i + 1) % 2]
-            return bank[:, 2 * C : 3 * C]
+            if EARLY <= i < E - 1:
+                return spare[1][:, (i - EARLY) * C : (i - EARLY + 1) * C]
+            return (gate_banks[(i + 2) % 3] if i < EARLY else spare[0])[:, 2 * C : 3 * C]
 
         def hidden(i):
             e = ORDER[i]
-            a, b = gate_banks[i % 3], lin_banks[i % 3]
-            first_layer(e, w1[e], s1c, s1h, a)
-            first_layer(e, w3[e], s3c, s3h, b)
+            a = gate_banks[i % 3]
+            passes = range(PASSES)
+            first_layer(e, [w1[e][:, s, :] for s in passes], [cold_rows(s1c, e, s) if e else s1h[:, s, :] for s in passes], a[:])
             gate = ring.tile([P, 2, P, 2], F32, name="gate")
-            nc.scalar.activation(gate[:], a[:].rearrange("j (p u v) -> j u p v", u=2, v=2), SIGMOID)
+            nc.scalar.activation(gate[:], paired(a[:]), SIGMOID)
             h = ring.tile([P, 2, P, 2], BF16, name="h", align_bytes=64)
-            nc.vector.tensor_tensor(h[:], b[:].rearrange("j (p u v) -> j u p v", u=2, v=2), gate[:], MULT)
+            if e:
+                b = lin_banks[i % 3]
+                first_layer(e, [w3[e][:, s, :] for s in passes], [cold_rows(s3c, e, s) for s in passes], b[:])
+                nc.vector.tensor_tensor(h[:], paired(b[:]), gate[:], MULT)
+                return h
+            for u in range(2):
+                b = lin_banks[(i + u) % 3][:, 0 : H // 2]
+                first_layer(e, [hot3[(s, u)] for s in passes], [s3h[:, s, u * H // 2 : (u + 1) * H // 2] for s in passes], b)
+                rows = slice(u * P // 2, (u + 1) * P // 2)
+                nc.vector.tensor_tensor(h[:, :, rows, :], paired(b), gate[:, :, rows, :], MULT)
             return h
 
         def turn(i, h):
@@ -173,8 +196,8 @@ def tile_moe_hot_s_glu_sigmoid_kernel(
                 ht[:].bitcast(F32).rearrange("p (j u) -> p j u", u=2),
                 turned_in(i).rearrange("p (u j) -> p j u", u=2),
             )
-            codes = ring.tile([P, C], U32, name="codes", align_bytes=64)
-            scales = ring.tile([P, C], U8, name="scales", align_bytes=64)
+            codes = held.tile([P, C], U32, name="codes%d" % i, align_bytes=64)
+            scales = held.tile([P, C], U8, name="scales%d" % i, align_bytes=64)
             nc.vector.quantize_mx(out=codes[:].bitcast(FP8X4), scales=scales[:], in_=ht[:])
             return codes, scales
 
@@ -182,7 +205,7 @@ def tile_moe_hot_s_glu_sigmoid_kernel(
             e = ORDER[i]
             nc.tensor.matmul_mx(
                 out=result_in(i),
-                lhsT=w2c[:, e - 1, :].bitcast(FP4X4) if e else w2h[:].bitcast(FP8X4),
+                lhsT=w2[e] if e else w2h[:].bitcast(FP8X4),
                 lhsT_scale=s2c[:, e - 1, :] if e else s2h[:, 0, :],
                 rhs=codes[:].bitcast(FP8X4),
                 rhs_scale=scales[:],
@@ -192,10 +215,15 @@ def tile_moe_hot_s_glu_sigmoid_kernel(
 
         def store(i):
             e = ORDER[i]
-            nc.scalar.copy(ysb[:, e * C : (e + 1) * C], result_in(i))
-            for first, end in GROUPS:
-                if e == end - 1:
-                    nc.sync.dma_start(out[:, first * C : end * C], ysb[:, first * C : end * C])
+            if EARLY <= i < E - 2:
+                return
+            first = {EARLY: 1, E - 1: EARLY + 1, 0: 0}.get(e)
+            if e == E - 1:
+                nc.vector.tensor_copy(ysb[:, first * C :], spare[1][:, 0 : (E - first) * C])
+            else:
+                nc.scalar.copy(ysb[:, e * C : (e + 1) * C], result_in(i))
+            if first is not None:
+                nc.sync.dma_start(out[:, first * C : (e + 1) * C], ysb[:, first * C : (e + 1) * C])
 
         hs = {}
         quantised = {}

@@ -117,14 +117,25 @@ def tile_moe_hot_s_glu_sigmoid_kernel(
         gw = held.tile([P, PASSES, AHEAD * C], U32, name="gw", align_bytes=64)
         gs = held.tile([P, PASSES, AHEAD * C], U8, name="gs", align_bytes=64)
 
+        home = {(e, s): (s, e - 1) for e in range(1, AHEAD + 1) for s in range(PASSES)}
+        after = {i: [] for i in range(E)}
+        waiting = [(e, s) for e in range(AHEAD + 1, E) for s in range(PASSES)]
+        for j, pair in enumerate(waiting):
+            home[pair] = home[(1 + j // 2, 1 + j % 2)]
+            after[j // 2].append(pair)
+        for s in range(PASSES):
+            home[(0, s)] = home[(AHEAD + 1, s)]
+            after[AHEAD].append((0, s))
+
         def columns(first, end, s):
-            place = ORDER.index(first) % AHEAD
-            return slice(place * C, (place + end - first) * C)
+            row, place = home[(first, s)]
+            return row, slice(place * C, (place + end - first) * C)
 
         def gather(first, end, s):
             entries = offsets[:, first * C // 16 : end * C // 16]
-            nc.vector.tensor_copy(gw[:, s, columns(first, end, s)], xw[s][:].bitcast(U32).indirect(entries))
-            nc.vector.tensor_copy(gs[:, s, columns(first, end, s)], xs[:, s, :].indirect(entries))
+            row, slots = columns(first, end, s)
+            nc.vector.tensor_copy(gw[:, row, slots], xw[s][:].bitcast(U32).indirect(entries))
+            nc.vector.tensor_copy(gs[:, row, slots], xs[:, s, :].indirect(entries))
 
         for first, end in GATHERS:
             for s in range(PASSES):
@@ -138,11 +149,11 @@ def tile_moe_hot_s_glu_sigmoid_kernel(
 
         def first_layer(e, words, scales, acc):
             for s in range(PASSES):
-                slots = columns(e, e + 1, s)
+                row, slots = columns(e, e + 1, s)
                 nc.tensor.matmul_mx(
                     out=acc,
-                    lhsT=gw[:, s, slots].bitcast(FP8X4),
-                    lhsT_scale=gs[:, s, slots],
+                    lhsT=gw[:, row, slots].bitcast(FP8X4),
+                    lhsT_scale=gs[:, row, slots],
                     rhs=words[s].bitcast(FP4X4 if e else FP8X4),
                     rhs_scale=scales[s],
                     start=(s == 0),
@@ -157,13 +168,13 @@ def tile_moe_hot_s_glu_sigmoid_kernel(
         spare = [psum.tile([P, H], F32, name="spare%d" % j) for j in range(2)]
 
         def turned_in(i):
-            bank = gate_banks[(i + 1) % 3] if i + 1 < E else spare[0]
+            bank = spare[0] if i == E - 2 else gate_banks[(i + 1) % 3]
             return bank[:, 0 : 2 * C]
 
         def result_in(i):
             if EARLY <= i < E - 1:
                 return spare[1][:, (i - EARLY) * C : (i - EARLY + 1) * C]
-            return (gate_banks[(i + 2) % 3] if i < EARLY else spare[0])[:, 2 * C : 3 * C]
+            return gate_banks[(i + 2) % 3][:, 2 * C : 3 * C]
 
         def hidden(i):
             e = ORDER[i]
@@ -237,6 +248,5 @@ def tile_moe_hot_s_glu_sigmoid_kernel(
                 quantised[i - 1] = quantise(i - 1)
             if i >= 2:
                 store(i - 2)
-            if i + AHEAD < E:
-                for s in range(PASSES):
-                    gather(ORDER[i + AHEAD], ORDER[i + AHEAD] + 1, s)
+            for e, s in after.get(i, []):
+                gather(e, e + 1, s)

@@ -22,9 +22,8 @@ MULT = mybir.AluOpType.mult
 
 ORDER = [1, 2, 3, 4, 5, 0]
 EARLY = 2
-GATHERS = [(1, 2), (2, 4)]
+GATHERS = [(1, 3), (3, 6), (0, 1)]
 SCALE_GROUPS = [(1, 4), (4, 6)]
-AHEAD = 3
 
 
 def tile_moe_hot_s_glu_sigmoid_kernel(
@@ -45,21 +44,22 @@ def tile_moe_hot_s_glu_sigmoid_kernel(
             engine.memset(t[:].rearrange("p a n -> p (a n)").bitcast(I32), 0)
             return t
 
-        xs = plane("xs", PASSES, T, nc.gpsimd)
+        xs = plane("xs", 1, T)
+        for s in range(PASSES):
+            (nc.scalar if s else nc.sync).dma_start(xs[:].bitcast(I32)[8 * s : 8 * s + 91 : 6, 0, :], x_scales.bitcast(I32)[s])
         s1c = {}
         s3c = {}
-        for first, end in SCALE_GROUPS:
+
+        def cold_planes(first, end):
             s1c[first] = plane("s1c%d" % first, (end - first) * PASSES, H)
             s3c[first] = plane("s3c%d" % first, (end - first) * PASSES, H)
-            if first == ORDER[0]:
-                s2c = plane("s2c", COLD, N)
-        s2h = plane("s2h", 1, N)
-        s1h = plane("s1h", PASSES, H)
-        s3h = plane("s3h", PASSES, H)
+
+        cold_planes(*SCALE_GROUPS[0])
+        gs = plane("gs", PASSES, E * C)
 
         def load_rows(t, src, r, queue=nc.sync):
             rows = src.rearrange("a (q r) n -> r q a n", r=4)[r]
-            queue.dma_start(t[:].bitcast(I32)[r:P:32, :, :], rows)
+            queue.dma_start(t[:, :, :].bitcast(I32)[r:P:32, :, :], rows)
 
         def flat(scales):
             return scales.bitcast(I32).rearrange("f s b n -> (f s) b n")
@@ -67,8 +67,32 @@ def tile_moe_hot_s_glu_sigmoid_kernel(
         xw = [held.tile([P, T], I32, name="xw%d" % s, align_bytes=64) for s in range(PASSES)]
         for s in range(PASSES):
             nc.sync.dma_start(xw[s][:], x_words[s].rearrange("p t d -> p (t d)").bitcast(I32))
+        packed = held.tile([P, E * C], U8, name="packed", align_bytes=64)
+        for half in range(2):
+            entries = offsets[:, half * E * C // 32 : (half + 1) * E * C // 32]
+            nc.vector.tensor_copy(packed[:, half * E * C // 2 : (half + 1) * E * C // 2], xs[:, 0, :].indirect(entries))
         for r in range(4):
-            load_rows(xs, x_scales.bitcast(I32), r, nc.scalar)
+            nc.scalar.dma_start(gs[:].bitcast(I32)[r:P:32, :, :], packed[:].bitcast(I32)[6 * r : 6 * r + 89 : 8, :])
+        s2c = plane("s2c", COLD, N)
+
+        gw = held.tile([P, PASSES, E * C], U32, name="gw", align_bytes=64)
+
+        def columns(first, end, s):
+            return s, slice(first * C, end * C)
+
+        def gather(first, end):
+            entries = offsets[:, first * C // 16 : end * C // 16]
+            for s in range(PASSES):
+                nc.vector.tensor_copy(gw[:, s, first * C : end * C], xw[s][:].bitcast(U32).indirect(entries))
+
+        for first, end in GATHERS:
+            gather(first, end)
+        s2h = plane("s2h", 1, N)
+        spent = [held.tile([P, 2 * PASSES, H], U8, name="xw%d" % s, align_bytes=64) for s in range(PASSES)]
+        s1c[SCALE_GROUPS[1][0]] = spent[0]
+        s3c[SCALE_GROUPS[1][0]] = spent[1]
+        s1h = spent[2][:, :PASSES, :]
+        s3h = spent[2][:, PASSES:, :]
         late = [(t, flat(src), r) for t, src in ((s1h, w1h_scales), (s3h, w3h_scales)) for r in range(4)]
 
         def load_second(first, end):
@@ -79,15 +103,15 @@ def tile_moe_hot_s_glu_sigmoid_kernel(
         w1 = {}
         w3 = {}
         for i, e in enumerate(ORDER[:-1]):
-            for first, end in SCALE_GROUPS:
-                if e == first:
-                    for t, src in ((s1c, w1c_scales), (s3c, w3c_scales)):
-                        for r in range(4):
-                            load_rows(t[e], flat(src[first - 1 : end - 1]), r)
             w1[e] = held.tile([P, PASSES, 2 * H], U8, name="w1_%d" % e, align_bytes=64)
             w3[e] = held.tile([P, PASSES, 2 * H], U8, name="w3_%d" % e, align_bytes=64)
             nc.sync.dma_start(w1[e][:].bitcast(I32), w1c_words[e - 1].rearrange("s p n -> p s n").bitcast(I32))
             nc.sync.dma_start(w3[e][:].bitcast(I32), w3c_words[e - 1].rearrange("s p n -> p s n").bitcast(I32))
+            for first, end in SCALE_GROUPS:
+                if e == max(first - 1, 1):
+                    for t, src in ((s1c, w1c_scales), (s3c, w3c_scales)):
+                        for r in range(4):
+                            load_rows(t[first], flat(src[first - 1 : end - 1]), r)
             if i == 1:
                 for r in range(4):
                     load_rows(s2c, flat(w2c_scales), r)
@@ -113,33 +137,6 @@ def tile_moe_hot_s_glu_sigmoid_kernel(
 
         ident = held.tile([P, P], F32, name="ident")
         make_identity(nc, ident[:])
-
-        gw = held.tile([P, PASSES, AHEAD * C], U32, name="gw", align_bytes=64)
-        gs = held.tile([P, PASSES, AHEAD * C], U8, name="gs", align_bytes=64)
-
-        home = {(e, s): (s, e - 1) for e in range(1, AHEAD + 1) for s in range(PASSES)}
-        after = {i: [] for i in range(E)}
-        waiting = [(e, s) for e in range(AHEAD + 1, E) for s in range(PASSES)]
-        for j, pair in enumerate(waiting):
-            home[pair] = home[(1 + j // 2, 1 + j % 2)]
-            after[j // 2].append(pair)
-        for s in range(PASSES):
-            home[(0, s)] = home[(AHEAD + 1, s)]
-            after[AHEAD].append((0, s))
-
-        def columns(first, end, s):
-            row, place = home[(first, s)]
-            return row, slice(place * C, (place + end - first) * C)
-
-        def gather(first, end, s):
-            entries = offsets[:, first * C // 16 : end * C // 16]
-            row, slots = columns(first, end, s)
-            nc.vector.tensor_copy(gw[:, row, slots], xw[s][:].bitcast(U32).indirect(entries))
-            nc.vector.tensor_copy(gs[:, row, slots], xs[:, s, :].indirect(entries))
-
-        for first, end in GATHERS:
-            for s in range(PASSES):
-                gather(first, end, s)
 
         ysb = held.tile([P, E * C], F32, name="ysb")
 
@@ -248,5 +245,3 @@ def tile_moe_hot_s_glu_sigmoid_kernel(
                 quantised[i - 1] = quantise(i - 1)
             if i >= 2:
                 store(i - 2)
-            for e, s in after.get(i, []):
-                gather(e, e + 1, s)

@@ -21,9 +21,7 @@ SIGMOID = mybir.ActivationFunctionType.Sigmoid
 MULT = mybir.AluOpType.mult
 
 ORDER = [1, 2, 3, 4, 5, 0]
-EARLY = 2
 GATHERS = [(1, 3), (3, 6), (0, 1)]
-SCALE_GROUPS = [(1, 4), (4, 6)]
 
 
 def tile_moe_hot_s_glu_sigmoid_kernel(
@@ -36,91 +34,85 @@ def tile_moe_hot_s_glu_sigmoid_kernel(
         ring = ctx.enter_context(tc.tile_pool(name="ring", bufs=3))
         psum = ctx.enter_context(tc.psum_pool(name="psum", bufs=1))
 
-        offsets = held.tile([P, E * C // 16], U16, name="offsets")
-        nc.sync.dma_start(offsets[:], offs)
-
-        def plane(name, rows, width, engine=nc.vector):
+        def zeroed(name, rows, width):
             t = held.tile([P, rows, width], U8, name=name, align_bytes=64)
-            engine.memset(t[:].rearrange("p a n -> p (a n)").bitcast(I32), 0)
+            nc.vector.memset(t[:].rearrange("p a n -> p (a n)").bitcast(I32), 0)
             return t
 
-        xs = plane("xs", 1, T)
+        def load_rows(t, scales):
+            rows = scales.bitcast(I32).rearrange("f s (q r) n -> r q (f s) n", r=4)
+            for r in range(4):
+                nc.sync.dma_start(t[:, :, :].bitcast(I32)[r:P:32, :, :], rows[r])
+
+        offsets = held.tile([P, E * C // 16], U16, name="offsets")
+        nc.sync.dma_start(offsets[:], offs)
+        xs = held.tile([P, 1, T], U8, name="xs", align_bytes=64)
+        nc.gpsimd.memset(xs[:].bitcast(I32), 0)
         for s in range(PASSES):
             (nc.scalar if s else nc.sync).dma_start(xs[:].bitcast(I32)[8 * s : 8 * s + 91 : 6, 0, :], x_scales.bitcast(I32)[s])
-        s1c = {}
-        s3c = {}
-
-        def cold_planes(first, end):
-            s1c[first] = plane("s1c%d" % first, (end - first) * PASSES, H)
-            s3c[first] = plane("s3c%d" % first, (end - first) * PASSES, H)
-
-        cold_planes(*SCALE_GROUPS[0])
-        gs = plane("gs", PASSES, E * C)
-
-        def load_rows(t, src, r, queue=nc.sync):
-            rows = src.rearrange("a (q r) n -> r q a n", r=4)[r]
-            queue.dma_start(t[:, :, :].bitcast(I32)[r:P:32, :, :], rows)
-
-        def flat(scales):
-            return scales.bitcast(I32).rearrange("f s b n -> (f s) b n")
-
+        s1_early = zeroed("s1_early", 3 * PASSES, H)
+        s3_early = zeroed("s3_early", 3 * PASSES, H)
+        gs = zeroed("gs", PASSES, E * C)
         xw = [held.tile([P, T], I32, name="xw%d" % s, align_bytes=64) for s in range(PASSES)]
         for s in range(PASSES):
             nc.sync.dma_start(xw[s][:], x_words[s].rearrange("p t d -> p (t d)").bitcast(I32))
-        packed = held.tile([P, E * C], U8, name="packed", align_bytes=64)
+
+        spread = held.tile([P, E * C], U8, name="spread", align_bytes=64)
         for half in range(2):
             entries = offsets[:, half * E * C // 32 : (half + 1) * E * C // 32]
-            nc.vector.tensor_copy(packed[:, half * E * C // 2 : (half + 1) * E * C // 2], xs[:, 0, :].indirect(entries))
-        for r in range(4):
-            nc.scalar.dma_start(gs[:].bitcast(I32)[r:P:32, :, :], packed[:].bitcast(I32)[6 * r : 6 * r + 89 : 8, :])
-        s2c = plane("s2c", COLD, N)
-
+            nc.vector.tensor_copy(spread[:, half * E * C // 2 : (half + 1) * E * C // 2], xs[:, 0, :].indirect(entries))
+        s2c = zeroed("s2c", COLD, N)
         gw = held.tile([P, PASSES, E * C], U32, name="gw", align_bytes=64)
-
-        def columns(first, end, s):
-            return s, slice(first * C, end * C)
-
-        def gather(first, end):
+        for first, end in GATHERS:
             entries = offsets[:, first * C // 16 : end * C // 16]
             for s in range(PASSES):
                 nc.vector.tensor_copy(gw[:, s, first * C : end * C], xw[s][:].bitcast(U32).indirect(entries))
+        s2h = zeroed("s2h", 1, N)
+        s1_late = held.tile([P, 2 * PASSES, H], U8, name="xw0", align_bytes=64)
+        s3_late = held.tile([P, 2 * PASSES, H], U8, name="xw1", align_bytes=64)
+        hot = held.tile([P, 2 * PASSES, H], U8, name="xw2", align_bytes=64)
+        s1_hot, s3_hot = hot[:, :PASSES, :], hot[:, PASSES:, :]
 
-        for first, end in GATHERS:
-            gather(first, end)
-        s2h = plane("s2h", 1, N)
-        spent = [held.tile([P, 2 * PASSES, H], U8, name="xw%d" % s, align_bytes=64) for s in range(PASSES)]
-        s1c[SCALE_GROUPS[1][0]] = spent[0]
-        s3c[SCALE_GROUPS[1][0]] = spent[1]
-        s1h = spent[2][:, :PASSES, :]
-        s3h = spent[2][:, PASSES:, :]
-        late = [(t, flat(src), r) for t, src in ((s1h, w1h_scales), (s3h, w3h_scales)) for r in range(4)]
+        def move(r, queue=nc.sync):
+            queue.dma_start(gs[:].bitcast(I32)[r:P:32, :, :], spread[:].bitcast(I32)[6 * r : 6 * r + 89 : 8, :])
+
+        w1, w3, w2 = {}, {}, {}
+
+        def load_cold(into, words, first, end):
+            t = held.tile([P, (end - first) * PASSES, 2 * H], U8, name="w%d_%d" % (1 if into is w1 else 3, first), align_bytes=64)
+            nc.sync.dma_start(t[:].bitcast(I32), words[first - 1 : end - 1].bitcast(I32).rearrange("f s p n -> p (f s) n"))
+            for e in range(first, end):
+                into[e] = [t[:, (e - first) * PASSES + s, :].bitcast(FP4X4) for s in range(PASSES)]
 
         def load_second(first, end):
             t = held.tile([P, end - first, 2 * N], U8, name="w2c%d" % first, align_bytes=64)
             nc.sync.dma_start(t[:].bitcast(I32), w2c_words[first - 1 : end - 1].bitcast(I32).rearrange("f s p n -> p (f s) n"))
-            return {e: t[:, e - first, :].bitcast(FP4X4) for e in range(first, end)}
+            for e in range(first, end):
+                w2[e] = t[:, e - first, :].bitcast(FP4X4)
 
-        w1 = {}
-        w3 = {}
-        for i, e in enumerate(ORDER[:-1]):
-            w1[e] = held.tile([P, PASSES, 2 * H], U8, name="w1_%d" % e, align_bytes=64)
-            w3[e] = held.tile([P, PASSES, 2 * H], U8, name="w3_%d" % e, align_bytes=64)
-            nc.sync.dma_start(w1[e][:].bitcast(I32), w1c_words[e - 1].rearrange("s p n -> p s n").bitcast(I32))
-            nc.sync.dma_start(w3[e][:].bitcast(I32), w3c_words[e - 1].rearrange("s p n -> p s n").bitcast(I32))
-            for first, end in SCALE_GROUPS:
-                if e == max(first - 1, 1):
-                    for t, src in ((s1c, w1c_scales), (s3c, w3c_scales)):
-                        for r in range(4):
-                            load_rows(t[first], flat(src[first - 1 : end - 1]), r)
-            if i == 1:
-                for r in range(4):
-                    load_rows(s2c, flat(w2c_scales), r)
-                w2 = load_second(1, EARLY + 1)
-            if i >= 3:
-                for item in late[4 * (i - 3) : 4 * (i - 2)]:
-                    load_rows(*item)
-        w1[0] = held.tile([P, PASSES, 4 * H], U8, name="w1_0", align_bytes=64)
-        nc.sync.dma_start(w1[0][:].bitcast(I32), w1h_words[0].rearrange("s p n d -> p s (n d)").bitcast(I32))
+        load_rows(s1_early, w1c_scales[0:3])
+        load_rows(s3_early, w3c_scales[0:3])
+        load_cold(w1, w1c_words, 1, 2)
+        move(0)
+        load_cold(w3, w3c_words, 1, 2)
+        move(1)
+        move(2)
+        move(3)
+        load_cold(w1, w1c_words, 2, 3)
+        load_cold(w3, w3c_words, 2, 3)
+        load_cold(w1, w1c_words, 3, 4)
+        load_cold(w3, w3c_words, 3, 4)
+        load_rows(s1_late, w1c_scales[3:5])
+        load_rows(s3_late, w3c_scales[3:5])
+        load_cold(w1, w1c_words, 4, 5)
+        load_cold(w3, w3c_words, 4, 5)
+        load_rows(s1_hot, w1h_scales)
+        load_cold(w1, w1c_words, 5, 6)
+        load_cold(w3, w3c_words, 5, 6)
+        w1h = held.tile([P, PASSES, 4 * H], U8, name="w1h", align_bytes=64)
+        nc.sync.dma_start(w1h[:].bitcast(I32), w1h_words[0].rearrange("s p n d -> p s (n d)").bitcast(I32))
+        w1[0] = [w1h[:, s, :].bitcast(FP8X4) for s in range(PASSES)]
+        load_rows(s3_hot, w3h_scales)
         hot3 = {}
         for s in range(PASSES):
             src = w3h_words[0, s].rearrange("p n d -> p (n d)").bitcast(I32)
@@ -128,30 +120,29 @@ def tile_moe_hot_s_glu_sigmoid_kernel(
                 t = held.tile([P, (end - first) * 2 * H], U8, name="w3h_%d_%d" % (s, first), align_bytes=64)
                 nc.sync.dma_start(t[:].bitcast(I32), src[:, first * H // 2 : end * H // 2])
                 for u in range(first, end):
-                    hot3[(s, u)] = t[:, (u - first) * 2 * H : (u - first + 1) * 2 * H]
-        w2.update(load_second(EARLY + 1, E))
+                    hot3[(s, u)] = t[:, (u - first) * 2 * H : (u - first + 1) * 2 * H].bitcast(FP8X4)
+        load_second(1, E)
+        load_rows(s2c, w2c_scales)
         w2h = held.tile([P, 4 * N], U8, name="w2h", align_bytes=64)
         nc.sync.dma_start(w2h[:].bitcast(I32), w2h_words[0, 0].rearrange("p n d -> p (n d)").bitcast(I32))
-        for r in range(4):
-            load_rows(s2h, flat(w2h_scales), r)
+        w2[0] = w2h[:].bitcast(FP8X4)
+        load_rows(s2h, w2h_scales)
 
         ident = held.tile([P, P], F32, name="ident")
         make_identity(nc, ident[:])
-
         ysb = held.tile([P, E * C], F32, name="ysb")
 
-        def cold_rows(planes, e, s):
-            first = max(f for f in planes if f <= e)
-            return planes[first][:, (e - first) * PASSES + s, :]
+        def cold_rows(early, late, e):
+            t, place = (early, e - 1) if e < 4 else (late, e - 4)
+            return [t[:, place * PASSES + s, :] for s in range(PASSES)]
 
         def first_layer(e, words, scales, acc):
             for s in range(PASSES):
-                row, slots = columns(e, e + 1, s)
                 nc.tensor.matmul_mx(
                     out=acc,
-                    lhsT=gw[:, row, slots].bitcast(FP8X4),
-                    lhsT_scale=gs[:, row, slots],
-                    rhs=words[s].bitcast(FP4X4 if e else FP8X4),
+                    lhsT=gw[:, s, e * C : (e + 1) * C].bitcast(FP8X4),
+                    lhsT_scale=gs[:, s, e * C : (e + 1) * C],
+                    rhs=words[s],
                     rhs_scale=scales[s],
                     start=(s == 0),
                     stop=(s == PASSES - 1),
@@ -165,30 +156,32 @@ def tile_moe_hot_s_glu_sigmoid_kernel(
         spare = [psum.tile([P, H], F32, name="spare%d" % j) for j in range(2)]
 
         def turned_in(i):
-            bank = spare[0] if i == E - 2 else gate_banks[(i + 1) % 3]
-            return bank[:, 0 : 2 * C]
+            if i < E - 2:
+                return gate_banks[(i | 1) + 1 - 3 * (i // 2)][:, i % 2 * 2 * C : (i % 2 + 1) * 2 * C]
+            return (spare[0] if i == E - 2 else gate_banks[0])[:, 0 : 2 * C]
 
         def result_in(i):
-            if EARLY <= i < E - 1:
-                return spare[1][:, (i - EARLY) * C : (i - EARLY + 1) * C]
-            return gate_banks[(i + 2) % 3][:, 2 * C : 3 * C]
+            if i < E - 2:
+                return spare[1][:, i * C : (i + 1) * C]
+            return (gate_banks[0] if ORDER[i] else lin_banks[1])[:, 2 * C : 3 * C]
 
         def hidden(i):
             e = ORDER[i]
             a = gate_banks[i % 3]
             passes = range(PASSES)
-            first_layer(e, [w1[e][:, s, :] for s in passes], [cold_rows(s1c, e, s) if e else s1h[:, s, :] for s in passes], a[:])
+            first_layer(e, w1[e], cold_rows(s1_early, s1_late, e) if e else [s1_hot[:, s, :] for s in passes], a[:])
             gate = ring.tile([P, 2, P, 2], F32, name="gate")
             nc.scalar.activation(gate[:], paired(a[:]), SIGMOID)
             h = ring.tile([P, 2, P, 2], BF16, name="h", align_bytes=64)
             if e:
                 b = lin_banks[i % 3]
-                first_layer(e, [w3[e][:, s, :] for s in passes], [cold_rows(s3c, e, s) for s in passes], b[:])
+                first_layer(e, w3[e], cold_rows(s3_early, s3_late, e), b[:])
                 nc.vector.tensor_tensor(h[:], paired(b[:]), gate[:], MULT)
                 return h
             for u in range(2):
                 b = lin_banks[(i + u) % 3][:, 0 : H // 2]
-                first_layer(e, [hot3[(s, u)] for s in passes], [s3h[:, s, u * H // 2 : (u + 1) * H // 2] for s in passes], b)
+                cols = slice(u * H // 2, (u + 1) * H // 2)
+                first_layer(e, [hot3[(s, u)] for s in passes], [s3_hot[:, s, cols] for s in passes], b)
                 rows = slice(u * P // 2, (u + 1) * P // 2)
                 nc.vector.tensor_tensor(h[:, :, rows, :], paired(b), gate[:, :, rows, :], MULT)
             return h
@@ -213,7 +206,7 @@ def tile_moe_hot_s_glu_sigmoid_kernel(
             e = ORDER[i]
             nc.tensor.matmul_mx(
                 out=result_in(i),
-                lhsT=w2[e] if e else w2h[:].bitcast(FP8X4),
+                lhsT=w2[e],
                 lhsT_scale=s2c[:, e - 1, :] if e else s2h[:, 0, :],
                 rhs=codes[:].bitcast(FP8X4),
                 rhs_scale=scales[:],
@@ -221,27 +214,22 @@ def tile_moe_hot_s_glu_sigmoid_kernel(
                 stop=True,
             )
 
-        def store(i):
-            e = ORDER[i]
-            if EARLY <= i < E - 2:
-                return
-            first = {EARLY: 1, E - 1: EARLY + 1, 0: 0}.get(e)
-            if e == E - 1:
-                nc.vector.tensor_copy(ysb[:, first * C :], spare[1][:, 0 : (E - first) * C])
-            else:
-                nc.scalar.copy(ysb[:, e * C : (e + 1) * C], result_in(i))
-            if first is not None:
-                nc.sync.dma_start(out[:, first * C : (e + 1) * C], ysb[:, first * C : (e + 1) * C])
-
         hs = {}
         quantised = {}
-        for i in range(E + 2):
+        for i in range(E + 1):
             if i < E:
                 hs[i] = hidden(i)
-            if i >= 2:
-                second_layer(i - 2, *quantised[i - 2])
-            if 1 <= i <= E:
-                turn(i - 1, hs[i - 1])
-                quantised[i - 1] = quantise(i - 1)
-            if i >= 2:
-                store(i - 2)
+            if i == E:
+                for j in range(COLD):
+                    second_layer(j, *quantised[j])
+                nc.vector.tensor_copy(ysb[:, C : COLD * C], spare[1][:])
+            ready = {2: [0, 1], 4: [2, 3], 5: [4], 6: [5]}.get(i, [])
+            for j in ready:
+                turn(j, hs[j])
+            for j in ready:
+                quantised[j] = quantise(j)
+        second_layer(COLD, *quantised[COLD])
+        nc.vector.tensor_copy(ysb[:, COLD * C :], result_in(COLD - 1))
+        nc.sync.dma_start(out[:, C:], ysb[:, C:])
+        nc.scalar.copy(ysb[:, :C], result_in(COLD))
+        nc.sync.dma_start(out[:, :C], ysb[:, :C])

@@ -20,8 +20,8 @@ FP4X4 = mybir.dt.float4_e2m1fn_x4
 SIGMOID = mybir.ActivationFunctionType.Sigmoid
 MULT = mybir.AluOpType.mult
 
-ORDER = [1, 2, 3, 4, 5, 0]
-GATHERS = [(1, 3), (3, 6), (0, 1)]
+ORDER = [3, 4, 5, 1, 2, 0]
+AHEAD = 3
 
 
 def tile_moe_hot_s_glu_sigmoid_kernel(
@@ -42,39 +42,23 @@ def tile_moe_hot_s_glu_sigmoid_kernel(
         def load_rows(t, scales):
             rows = scales.bitcast(I32).rearrange("f s (q r) n -> r q (f s) n", r=4)
             for r in range(4):
-                nc.sync.dma_start(t[:, :, :].bitcast(I32)[r:P:32, :, :], rows[r])
+                nc.sync.dma_start(t[:].bitcast(I32)[r:P:32, :, :], rows[r])
 
         offsets = held.tile([P, E * C // 16], U16, name="offsets")
         nc.sync.dma_start(offsets[:], offs)
-        xs = held.tile([P, 1, T], U8, name="xs", align_bytes=64)
-        nc.gpsimd.memset(xs[:].bitcast(I32), 0)
-        for s in range(PASSES):
-            (nc.scalar if s else nc.sync).dma_start(xs[:].bitcast(I32)[8 * s : 8 * s + 91 : 6, 0, :], x_scales.bitcast(I32)[s])
+        xs = held.tile([P, PASSES, T], U8, name="xs", align_bytes=64)
+        nc.gpsimd.memset(xs[:].rearrange("p a n -> p (a n)").bitcast(I32), 0)
         s1_early = zeroed("s1_early", 3 * PASSES, H)
         s3_early = zeroed("s3_early", 3 * PASSES, H)
-        gs = zeroed("gs", PASSES, E * C)
+        s1_late = zeroed("s1_late", 2 * PASSES, H)
+        s3_late = zeroed("s3_late", 2 * PASSES, H)
         xw = [held.tile([P, T], I32, name="xw%d" % s, align_bytes=64) for s in range(PASSES)]
+        token_rows = x_scales.bitcast(I32).rearrange("s (q r) n -> r q s n", r=4)
         for s in range(PASSES):
             nc.sync.dma_start(xw[s][:], x_words[s].rearrange("p t d -> p (t d)").bitcast(I32))
-
-        spread = held.tile([P, E * C], U8, name="spread", align_bytes=64)
-        for half in range(2):
-            entries = offsets[:, half * E * C // 32 : (half + 1) * E * C // 32]
-            nc.vector.tensor_copy(spread[:, half * E * C // 2 : (half + 1) * E * C // 2], xs[:, 0, :].indirect(entries))
-        s2c = zeroed("s2c", COLD, N)
-        gw = held.tile([P, PASSES, E * C], U32, name="gw", align_bytes=64)
-        for first, end in GATHERS:
-            entries = offsets[:, first * C // 16 : end * C // 16]
-            for s in range(PASSES):
-                nc.vector.tensor_copy(gw[:, s, first * C : end * C], xw[s][:].bitcast(U32).indirect(entries))
-        s2h = zeroed("s2h", 1, N)
-        s1_late = held.tile([P, 2 * PASSES, H], U8, name="xw0", align_bytes=64)
-        s3_late = held.tile([P, 2 * PASSES, H], U8, name="xw1", align_bytes=64)
-        hot = held.tile([P, 2 * PASSES, H], U8, name="xw2", align_bytes=64)
-        s1_hot, s3_hot = hot[:, :PASSES, :], hot[:, PASSES:, :]
-
-        def move(r, queue=nc.sync):
-            queue.dma_start(gs[:].bitcast(I32)[r:P:32, :, :], spread[:].bitcast(I32)[6 * r : 6 * r + 89 : 8, :])
+            if s == 0:
+                for r in range(4):
+                    nc.sync.dma_start(xs[:].bitcast(I32)[r:P:32, :, :], token_rows[r])
 
         w1, w3, w2 = {}, {}, {}
 
@@ -90,58 +74,57 @@ def tile_moe_hot_s_glu_sigmoid_kernel(
             for e in range(first, end):
                 w2[e] = t[:, e - first, :].bitcast(FP4X4)
 
-        load_rows(s1_early, w1c_scales[0:3])
-        load_rows(s3_early, w3c_scales[0:3])
-        load_cold(w1, w1c_words, 1, 2)
-        move(0)
-        load_cold(w3, w3c_words, 1, 2)
-        move(1)
-        move(2)
-        move(3)
-        load_cold(w1, w1c_words, 2, 3)
-        load_cold(w3, w3c_words, 2, 3)
+        load_rows(s1_early, w1c_scales[2:5])
+        load_rows(s3_early, w3c_scales[2:5])
         load_cold(w1, w1c_words, 3, 4)
         load_cold(w3, w3c_words, 3, 4)
-        load_rows(s1_late, w1c_scales[3:5])
-        load_rows(s3_late, w3c_scales[3:5])
         load_cold(w1, w1c_words, 4, 5)
         load_cold(w3, w3c_words, 4, 5)
-        load_rows(s1_hot, w1h_scales)
         load_cold(w1, w1c_words, 5, 6)
         load_cold(w3, w3c_words, 5, 6)
-        w1h = held.tile([P, PASSES, 4 * H], U8, name="w1h", align_bytes=64)
-        nc.sync.dma_start(w1h[:].bitcast(I32), w1h_words[0].rearrange("s p n d -> p s (n d)").bitcast(I32))
-        w1[0] = [w1h[:, s, :].bitcast(FP8X4) for s in range(PASSES)]
-        load_rows(s3_hot, w3h_scales)
-        hot3 = {}
-        for s in range(PASSES):
-            src = w3h_words[0, s].rearrange("p n d -> p (n d)").bitcast(I32)
-            for first, end in [(0, 2)] if s < PASSES - 1 else [(0, 1), (1, 2)]:
-                t = held.tile([P, (end - first) * 2 * H], U8, name="w3h_%d_%d" % (s, first), align_bytes=64)
-                nc.sync.dma_start(t[:].bitcast(I32), src[:, first * H // 2 : end * H // 2])
-                for u in range(first, end):
-                    hot3[(s, u)] = t[:, (u - first) * 2 * H : (u - first + 1) * 2 * H].bitcast(FP8X4)
-        load_second(1, E)
-        load_rows(s2c, w2c_scales)
-        w2h = held.tile([P, 4 * N], U8, name="w2h", align_bytes=64)
-        nc.sync.dma_start(w2h[:].bitcast(I32), w2h_words[0, 0].rearrange("p n d -> p (n d)").bitcast(I32))
-        w2[0] = w2h[:].bitcast(FP8X4)
-        load_rows(s2h, w2h_scales)
+        load_rows(s1_late, w1c_scales[0:2])
+        load_rows(s3_late, w3c_scales[0:2])
+        load_cold(w1, w1c_words, 1, 2)
+        load_cold(w3, w3c_words, 1, 2)
 
         ident = held.tile([P, P], F32, name="ident")
         make_identity(nc, ident[:])
         ysb = held.tile([P, E * C], F32, name="ysb")
 
+        gw = held.tile([P, PASSES, COLD * C], U32, name="gw", align_bytes=64)
+        gs = held.tile([P, PASSES, AHEAD * C], U8, name="gs", align_bytes=64)
+
+        def entries(first, end):
+            return offsets[:, first * C // 16 : end * C // 16]
+
+        def place(e):
+            return ORDER.index(e) % AHEAD * C
+
+        def word_place(e):
+            return ((e or ORDER[AHEAD - 1]) - 1) * C
+
+        def gather_words(first, end, s):
+            nc.vector.tensor_copy(gw[:, s, word_place(first) : word_place(first) + (end - first) * C], xw[s][:].bitcast(U32).indirect(entries(first, end)))
+
+        def gather_scales(first, end, s):
+            nc.vector.tensor_copy(gs[:, s, place(first) : place(first) + (end - first) * C], xs[:, s, :].indirect(entries(first, end)))
+
+        for s in range(PASSES):
+            gather_words(AHEAD, E, s)
+            gather_scales(AHEAD, E, s)
+        for s in range(PASSES):
+            gather_words(1, AHEAD, s)
+
         def cold_rows(early, late, e):
-            t, place = (early, e - 1) if e < 4 else (late, e - 4)
+            t, place = (early, e - 3) if e >= 3 else (late, e - 1)
             return [t[:, place * PASSES + s, :] for s in range(PASSES)]
 
         def first_layer(e, words, scales, acc):
             for s in range(PASSES):
                 nc.tensor.matmul_mx(
                     out=acc,
-                    lhsT=gw[:, s, e * C : (e + 1) * C].bitcast(FP8X4),
-                    lhsT_scale=gs[:, s, e * C : (e + 1) * C],
+                    lhsT=gw[:, s, word_place(e) : word_place(e) + C].bitcast(FP8X4),
+                    lhsT_scale=gs[:, s, place(e) : place(e) + C],
                     rhs=words[s],
                     rhs_scale=scales[s],
                     start=(s == 0),
@@ -161,9 +144,10 @@ def tile_moe_hot_s_glu_sigmoid_kernel(
             return (spare[0] if i == E - 2 else gate_banks[0])[:, 0 : 2 * C]
 
         def result_in(i):
-            if i < E - 2:
-                return spare[1][:, i * C : (i + 1) * C]
-            return (gate_banks[0] if ORDER[i] else lin_banks[1])[:, 2 * C : 3 * C]
+            e = ORDER[i]
+            if e >= 2:
+                return spare[1][:, (e - 2) * C : (e - 1) * C]
+            return (gate_banks[0] if e else lin_banks[1])[:, 2 * C : 3 * C]
 
         def hidden(i):
             e = ORDER[i]
@@ -214,22 +198,56 @@ def tile_moe_hot_s_glu_sigmoid_kernel(
                 stop=True,
             )
 
-        hs = {}
+        hs = {i: hidden(i) for i in range(2)}
+
+        s1_hot = held.tile([P, PASSES, H], U8, name="w1_%d" % ORDER[0], align_bytes=64)
+        s3_hot = held.tile([P, PASSES, H], U8, name="w3_%d" % ORDER[0], align_bytes=64)
+        s2c = held.tile([P, COLD, N], U8, name="w1_%d" % ORDER[1], align_bytes=64)
+        s2h = held.tile([P, 1, N], U8, name="w3_%d" % ORDER[1], align_bytes=64)
+        load_rows(s1_hot, w1h_scales)
+        load_cold(w1, w1c_words, 2, 3)
+        load_cold(w3, w3c_words, 2, 3)
+        w1h = held.tile([P, PASSES, 4 * H], U8, name="w1h", align_bytes=64)
+        nc.sync.dma_start(w1h[:].bitcast(I32), w1h_words[0].rearrange("s p n d -> p s (n d)").bitcast(I32))
+        w1[0] = [w1h[:, s, :].bitcast(FP8X4) for s in range(PASSES)]
+        load_rows(s3_hot, w3h_scales)
+        hot3 = {}
+        for s in range(PASSES):
+            src = w3h_words[0, s].rearrange("p n d -> p (n d)").bitcast(I32)
+            for first, end in [(0, 2)] if s < PASSES - 1 else [(0, 1), (1, 2)]:
+                t = held.tile([P, (end - first) * 2 * H], U8, name="w3h_%d_%d" % (s, first), align_bytes=64)
+                nc.sync.dma_start(t[:].bitcast(I32), src[:, first * H // 2 : end * H // 2])
+                for u in range(first, end):
+                    hot3[(s, u)] = t[:, (u - first) * 2 * H : (u - first + 1) * 2 * H].bitcast(FP8X4)
+        load_second(1, E)
+        load_rows(s2c, w2c_scales)
+        w2h = held.tile([P, 4 * N], U8, name="w2h", align_bytes=64)
+        nc.sync.dma_start(w2h[:].bitcast(I32), w2h_words[0, 0].rearrange("p n d -> p (n d)").bitcast(I32))
+        w2[0] = w2h[:].bitcast(FP8X4)
+        load_rows(s2h, w2h_scales)
+
         quantised = {}
         for i in range(E + 1):
-            if i < E:
+            if 2 <= i < E:
                 hs[i] = hidden(i)
             if i == E:
-                for j in range(COLD):
-                    second_layer(j, *quantised[j])
-                nc.vector.tensor_copy(ysb[:, C : COLD * C], spare[1][:])
+                for e in range(COLD, 0, -1):
+                    second_layer(ORDER.index(e), *quantised[ORDER.index(e)])
+                nc.vector.tensor_copy(ysb[:, 2 * C :], spare[1][:])
+                nc.sync.dma_start(out[:, 2 * C :], ysb[:, 2 * C :])
             ready = {2: [0, 1], 4: [2, 3], 5: [4], 6: [5]}.get(i, [])
             for j in ready:
                 turn(j, hs[j])
             for j in ready:
                 quantised[j] = quantise(j)
+            if i < E - AHEAD:
+                late = ORDER[i + AHEAD]
+                for s in range(PASSES):
+                    if late == 0:
+                        gather_words(late, late + 1, s)
+                    gather_scales(late, late + 1, s)
         second_layer(COLD, *quantised[COLD])
-        nc.vector.tensor_copy(ysb[:, COLD * C :], result_in(COLD - 1))
-        nc.sync.dma_start(out[:, C:], ysb[:, C:])
+        nc.vector.tensor_copy(ysb[:, C : 2 * C], result_in(ORDER.index(1)))
+        nc.sync.dma_start(out[:, C : 2 * C], ysb[:, C : 2 * C])
         nc.scalar.copy(ysb[:, :C], result_in(COLD))
         nc.sync.dma_start(out[:, :C], ysb[:, :C])

@@ -45,18 +45,19 @@ def tile_moe_hot_s_glu_sigmoid_kernel(
                 nc.sync.dma_start(t[:].bitcast(I32)[r:P:32, :, :], rows[r])
 
         offsets = held.tile([P, E * C // 16], U16, name="offsets")
-        nc.sync.dma_start(offsets[:], offs)
         xs = held.tile([P, PASSES, T], U8, name="xs", align_bytes=64)
         nc.gpsimd.memset(xs[:].rearrange("p a n -> p (a n)").bitcast(I32), 0)
         s1_early = zeroed("s1_early", 3 * PASSES, H)
         s3_early = zeroed("s3_early", 3 * PASSES, H)
         s1_late = zeroed("s1_late", 2 * PASSES, H)
         s3_late = zeroed("s3_late", 2 * PASSES, H)
+        s2h = zeroed("s2h", 1, N)
         xw = [held.tile([P, T], I32, name="xw%d" % s, align_bytes=64) for s in range(PASSES)]
         token_rows = x_scales.bitcast(I32).rearrange("s (q r) n -> r q s n", r=4)
         for s in range(PASSES):
             nc.sync.dma_start(xw[s][:], x_words[s].rearrange("p t d -> p (t d)").bitcast(I32))
             if s == 0:
+                nc.sync.dma_start(offsets[:], offs)
                 for r in range(4):
                     nc.sync.dma_start(xs[:].bitcast(I32)[r:P:32, :, :], token_rows[r])
 
@@ -80,6 +81,7 @@ def tile_moe_hot_s_glu_sigmoid_kernel(
         load_cold(w3, w3c_words, 3, 4)
         load_cold(w1, w1c_words, 4, 5)
         load_cold(w3, w3c_words, 4, 5)
+        load_rows(s2h, w2h_scales)
         load_cold(w1, w1c_words, 5, 6)
         load_cold(w3, w3c_words, 5, 6)
         load_rows(s1_late, w1c_scales[0:2])
@@ -147,7 +149,7 @@ def tile_moe_hot_s_glu_sigmoid_kernel(
             e = ORDER[i]
             if e >= 2:
                 return spare[1][:, (e - 2) * C : (e - 1) * C]
-            return (gate_banks[0] if e else lin_banks[1])[:, 2 * C : 3 * C]
+            return (lin_banks[1] if e else spare[0])[:, 2 * C : 3 * C]
 
         def hidden(i):
             e = ORDER[i]
@@ -203,14 +205,13 @@ def tile_moe_hot_s_glu_sigmoid_kernel(
         s1_hot = held.tile([P, PASSES, H], U8, name="w1_%d" % ORDER[0], align_bytes=64)
         s3_hot = held.tile([P, PASSES, H], U8, name="w3_%d" % ORDER[0], align_bytes=64)
         s2c = held.tile([P, COLD, N], U8, name="w1_%d" % ORDER[1], align_bytes=64)
-        s2h = held.tile([P, 1, N], U8, name="w3_%d" % ORDER[1], align_bytes=64)
         load_rows(s1_hot, w1h_scales)
         load_cold(w1, w1c_words, 2, 3)
         load_cold(w3, w3c_words, 2, 3)
+        load_rows(s3_hot, w3h_scales)
         w1h = held.tile([P, PASSES, 4 * H], U8, name="w1h", align_bytes=64)
         nc.sync.dma_start(w1h[:].bitcast(I32), w1h_words[0].rearrange("s p n d -> p s (n d)").bitcast(I32))
         w1[0] = [w1h[:, s, :].bitcast(FP8X4) for s in range(PASSES)]
-        load_rows(s3_hot, w3h_scales)
         hot3 = {}
         for s in range(PASSES):
             src = w3h_words[0, s].rearrange("p n d -> p (n d)").bitcast(I32)
@@ -224,17 +225,11 @@ def tile_moe_hot_s_glu_sigmoid_kernel(
         w2h = held.tile([P, 4 * N], U8, name="w2h", align_bytes=64)
         nc.sync.dma_start(w2h[:].bitcast(I32), w2h_words[0, 0].rearrange("p n d -> p (n d)").bitcast(I32))
         w2[0] = w2h[:].bitcast(FP8X4)
-        load_rows(s2h, w2h_scales)
 
         quantised = {}
         for i in range(E + 1):
             if 2 <= i < E:
                 hs[i] = hidden(i)
-            if i == E:
-                for e in range(COLD, 0, -1):
-                    second_layer(ORDER.index(e), *quantised[ORDER.index(e)])
-                nc.vector.tensor_copy(ysb[:, 2 * C :], spare[1][:])
-                nc.sync.dma_start(out[:, 2 * C :], ysb[:, 2 * C :])
             ready = {2: [0, 1], 4: [2, 3], 5: [4], 6: [5]}.get(i, [])
             for j in ready:
                 turn(j, hs[j])
@@ -246,6 +241,10 @@ def tile_moe_hot_s_glu_sigmoid_kernel(
                     if late == 0:
                         gather_words(late, late + 1, s)
                     gather_scales(late, late + 1, s)
+        for e in range(COLD, 0, -1):
+            second_layer(ORDER.index(e), *quantised[ORDER.index(e)])
+        nc.scalar.copy(ysb[:, 2 * C :], spare[1][:])
+        nc.sync.dma_start(out[:, 2 * C :], ysb[:, 2 * C :])
         second_layer(COLD, *quantised[COLD])
         nc.vector.tensor_copy(ysb[:, C : 2 * C], result_in(ORDER.index(1)))
         nc.sync.dma_start(out[:, C : 2 * C], ysb[:, C : 2 * C])

@@ -52,14 +52,8 @@ def tile_moe_hot_s_glu_sigmoid_kernel(
         s1_late = zeroed("s1_late", 2 * PASSES, H)
         s3_late = zeroed("s3_late", 2 * PASSES, H)
         s2h = zeroed("s2h", 1, N)
-        xw = [held.tile([P, T], I32, name="xw%d" % s, align_bytes=64) for s in range(PASSES)]
         token_rows = x_scales.bitcast(I32).rearrange("s (q r) n -> r q s n", r=4)
-        for s in range(PASSES):
-            nc.sync.dma_start(xw[s][:], x_words[s].rearrange("p t d -> p (t d)").bitcast(I32))
-            if s == 0:
-                nc.sync.dma_start(offsets[:], offs)
-                for r in range(4):
-                    nc.sync.dma_start(xs[:].bitcast(I32)[r:P:32, :, :], token_rows[r])
+        xw = held.tile([P, PASSES, T], I32, name="xw", align_bytes=64)
 
         w1, w3, w2 = {}, {}, {}
 
@@ -75,13 +69,16 @@ def tile_moe_hot_s_glu_sigmoid_kernel(
             for e in range(first, end):
                 w2[e] = t[:, e - first, :].bitcast(FP4X4)
 
+        load_cold(w1, w1c_words, 3, 4)
+        nc.sync.dma_start(offsets[:], offs)
+        for r in range(4):
+            nc.sync.dma_start(xs[:].bitcast(I32)[r:P:32, :, :], token_rows[r])
+        nc.sync.dma_start(xw[:], x_words.rearrange("s p t d -> p s (t d)").bitcast(I32))
         load_rows(s1_early, w1c_scales[2:5])
         load_rows(s3_early, w3c_scales[2:5])
-        load_cold(w1, w1c_words, 3, 4)
         load_cold(w3, w3c_words, 3, 4)
         load_cold(w1, w1c_words, 4, 5)
         load_cold(w3, w3c_words, 4, 5)
-        load_rows(s2h, w2h_scales)
         load_cold(w1, w1c_words, 5, 6)
         load_cold(w3, w3c_words, 5, 6)
         load_rows(s1_late, w1c_scales[0:2])
@@ -106,14 +103,16 @@ def tile_moe_hot_s_glu_sigmoid_kernel(
             return ((e or ORDER[AHEAD - 1]) - 1) * C
 
         def gather_words(first, end, s):
-            nc.vector.tensor_copy(gw[:, s, word_place(first) : word_place(first) + (end - first) * C], xw[s][:].bitcast(U32).indirect(entries(first, end)))
+            nc.vector.tensor_copy(gw[:, s, word_place(first) : word_place(first) + (end - first) * C], xw[:, s, :].bitcast(U32).indirect(entries(first, end)))
 
         def gather_scales(first, end, s):
             nc.vector.tensor_copy(gs[:, s, place(first) : place(first) + (end - first) * C], xs[:, s, :].indirect(entries(first, end)))
 
-        for s in range(PASSES):
-            gather_words(AHEAD, E, s)
-            gather_scales(AHEAD, E, s)
+        for first, end in [(AHEAD, AHEAD + 1), (AHEAD + 1, E)]:
+            for s in range(PASSES):
+                gather_scales(first, end, s)
+            for s in range(PASSES):
+                gather_words(first, end, s)
         for s in range(PASSES):
             gather_words(1, AHEAD, s)
 
@@ -225,6 +224,7 @@ def tile_moe_hot_s_glu_sigmoid_kernel(
         w2h = held.tile([P, 4 * N], U8, name="w2h", align_bytes=64)
         nc.sync.dma_start(w2h[:].bitcast(I32), w2h_words[0, 0].rearrange("p n d -> p (n d)").bitcast(I32))
         w2[0] = w2h[:].bitcast(FP8X4)
+        load_rows(s2h, w2h_scales)
 
         quantised = {}
         for i in range(E + 1):

@@ -49,9 +49,6 @@ def tile_moe_hot_s_glu_sigmoid_kernel(
         nc.gpsimd.memset(xs[:].rearrange("p a n -> p (a n)").bitcast(I32), 0)
         s1_early = zeroed("s1_early", 3 * PASSES, H)
         s3_early = zeroed("s3_early", 3 * PASSES, H)
-        s1_late = zeroed("s1_late", 2 * PASSES, H)
-        s3_late = zeroed("s3_late", 2 * PASSES, H)
-        s2h = zeroed("s2h", 1, N)
         token_rows = x_scales.bitcast(I32).rearrange("s (q r) n -> r q s n", r=4)
         xw = held.tile([P, PASSES, T], I32, name="xw", align_bytes=64)
 
@@ -81,10 +78,6 @@ def tile_moe_hot_s_glu_sigmoid_kernel(
         load_cold(w3, w3c_words, 4, 5)
         load_cold(w1, w1c_words, 5, 6)
         load_cold(w3, w3c_words, 5, 6)
-        load_rows(s1_late, w1c_scales[0:2])
-        load_rows(s3_late, w3c_scales[0:2])
-        load_cold(w1, w1c_words, 1, 2)
-        load_cold(w3, w3c_words, 1, 2)
 
         ident = held.tile([P, P], F32, name="ident")
         make_identity(nc, ident[:])
@@ -116,8 +109,11 @@ def tile_moe_hot_s_glu_sigmoid_kernel(
         for s in range(PASSES):
             gather_words(1, AHEAD, s)
 
-        def cold_rows(early, late, e):
-            t, place = (early, e - 3) if e >= 3 else (late, e - 1)
+        def cold_rows(matrix, e):
+            if e >= 3:
+                t, place = (s1_early if matrix == 1 else s3_early), e - 3
+            else:
+                t, place = (s1_late if matrix == 1 else s3_late), e - 1
             return [t[:, place * PASSES + s, :] for s in range(PASSES)]
 
         def first_layer(e, words, scales, acc):
@@ -154,13 +150,13 @@ def tile_moe_hot_s_glu_sigmoid_kernel(
             e = ORDER[i]
             a = gate_banks[i % 3]
             passes = range(PASSES)
-            first_layer(e, w1[e], cold_rows(s1_early, s1_late, e) if e else [s1_hot[:, s, :] for s in passes], a[:])
+            first_layer(e, w1[e], cold_rows(1, e) if e else [s1_hot[:, s, :] for s in passes], a[:])
             gate = ring.tile([P, 2, P, 2], F32, name="gate")
             nc.scalar.activation(gate[:], paired(a[:]), SIGMOID)
             h = ring.tile([P, 2, P, 2], BF16, name="h", align_bytes=64)
             if e:
                 b = lin_banks[i % 3]
-                first_layer(e, w3[e], cold_rows(s3_early, s3_late, e), b[:])
+                first_layer(e, w3[e], cold_rows(3, e), b[:])
                 nc.vector.tensor_tensor(h[:], paired(b[:]), gate[:], MULT)
                 return h
             for u in range(2):
@@ -199,11 +195,21 @@ def tile_moe_hot_s_glu_sigmoid_kernel(
                 stop=True,
             )
 
-        hs = {i: hidden(i) for i in range(2)}
+        hs = {i: hidden(i) for i in range(AHEAD)}
 
-        s1_hot = held.tile([P, PASSES, H], U8, name="w1_%d" % ORDER[0], align_bytes=64)
-        s3_hot = held.tile([P, PASSES, H], U8, name="w3_%d" % ORDER[0], align_bytes=64)
-        s2c = held.tile([P, COLD, N], U8, name="w1_%d" % ORDER[1], align_bytes=64)
+        def spent(matrix, i, rows, width):
+            return held.tile([P, rows, width], U8, name="w%d_%d" % (matrix, ORDER[i]), align_bytes=64)
+
+        s1_late = spent(1, 0, 2 * PASSES, H)
+        s3_late = spent(3, 0, 2 * PASSES, H)
+        s1_hot = spent(1, 1, PASSES, H)
+        s3_hot = spent(3, 1, PASSES, H)
+        s2c = spent(1, 2, COLD, N)
+        s2h = spent(3, 2, 1, N)
+        load_rows(s1_late, w1c_scales[0:2])
+        load_rows(s3_late, w3c_scales[0:2])
+        load_cold(w1, w1c_words, 1, 2)
+        load_cold(w3, w3c_words, 1, 2)
         load_rows(s1_hot, w1h_scales)
         load_cold(w1, w1c_words, 2, 3)
         load_cold(w3, w3c_words, 2, 3)
@@ -228,7 +234,7 @@ def tile_moe_hot_s_glu_sigmoid_kernel(
 
         quantised = {}
         for i in range(E + 1):
-            if 2 <= i < E:
+            if AHEAD <= i < E:
                 hs[i] = hidden(i)
             ready = {2: [0, 1], 4: [2, 3], 5: [4], 6: [5]}.get(i, [])
             for j in ready:

@@ -83,31 +83,26 @@ def tile_moe_hot_s_glu_sigmoid_kernel(
         make_identity(nc, ident[:])
         ysb = held.tile([P, E * C], F32, name="ysb")
 
-        gw = held.tile([P, PASSES, COLD * C], U32, name="gw", align_bytes=64)
+        gw = held.tile([P, PASSES, E * C], U32, name="gw", align_bytes=64)
         gs = held.tile([P, PASSES, AHEAD * C], U8, name="gs", align_bytes=64)
 
         def entries(first, end):
             return offsets[:, first * C // 16 : end * C // 16]
 
-        def place(e):
-            return ORDER.index(e) % AHEAD * C
-
-        def word_place(e):
-            return ((e or ORDER[AHEAD - 1]) - 1) * C
-
-        def gather_words(first, end, s):
-            nc.vector.tensor_copy(gw[:, s, word_place(first) : word_place(first) + (end - first) * C], xw[:, s, :].bitcast(U32).indirect(entries(first, end)))
-
-        def gather_scales(first, end, s):
-            nc.vector.tensor_copy(gs[:, s, place(first) : place(first) + (end - first) * C], xs[:, s, :].indirect(entries(first, end)))
-
-        for first, end in [(AHEAD, AHEAD + 1), (AHEAD + 1, E)]:
+        def gather_words(first, end):
             for s in range(PASSES):
-                gather_scales(first, end, s)
+                nc.vector.tensor_copy(gw[:, s, first * C : end * C], xw[:, s, :].bitcast(U32).indirect(entries(first, end)))
+
+        def gather_scales(into, first, end):
             for s in range(PASSES):
-                gather_words(first, end, s)
-        for s in range(PASSES):
-            gather_words(1, AHEAD, s)
+                nc.vector.tensor_copy(into[:, s, :], xs[:, s, :].indirect(entries(first, end)))
+
+        gather_scales(gs, AHEAD, E)
+        gather_words(AHEAD, AHEAD + 1)
+        gather_words(AHEAD + 1, E)
+        gather_words(0, AHEAD)
+        gs_late = held.tile([P, PASSES, AHEAD * C], U8, name="xw", align_bytes=64)
+        gather_scales(gs_late, 0, AHEAD)
 
         def cold_rows(matrix, e):
             if e >= 3:
@@ -120,8 +115,8 @@ def tile_moe_hot_s_glu_sigmoid_kernel(
             for s in range(PASSES):
                 nc.tensor.matmul_mx(
                     out=acc,
-                    lhsT=gw[:, s, word_place(e) : word_place(e) + C].bitcast(FP8X4),
-                    lhsT_scale=gs[:, s, place(e) : place(e) + C],
+                    lhsT=gw[:, s, e * C : (e + 1) * C].bitcast(FP8X4),
+                    lhsT_scale=(gs if e >= AHEAD else gs_late)[:, s, e % AHEAD * C : (e % AHEAD + 1) * C],
                     rhs=words[s],
                     rhs_scale=scales[s],
                     start=(s == 0),
@@ -241,12 +236,6 @@ def tile_moe_hot_s_glu_sigmoid_kernel(
                 turn(j, hs[j])
             for j in ready:
                 quantised[j] = quantise(j)
-            if i < E - AHEAD:
-                late = ORDER[i + AHEAD]
-                for s in range(PASSES):
-                    if late == 0:
-                        gather_words(late, late + 1, s)
-                    gather_scales(late, late + 1, s)
         for e in range(COLD, 0, -1):
             second_layer(ORDER.index(e), *quantised[ORDER.index(e)])
         nc.scalar.copy(ysb[:, 2 * C :], spare[1][:])

@@ -34,21 +34,22 @@ def tile_moe_hot_s_glu_sigmoid_kernel(
         ring = ctx.enter_context(tc.tile_pool(name="ring", bufs=3))
         psum = ctx.enter_context(tc.psum_pool(name="psum", bufs=1))
 
-        def zeroed(name, rows, width):
-            t = held.tile([P, rows, width], U8, name=name, align_bytes=64)
-            nc.vector.memset(t[:].rearrange("p a n -> p (a n)").bitcast(I32), 0)
-            return t
-
-        def load_rows(t, scales):
+        def load_rows(t, scales, queue=nc.sync):
             rows = scales.bitcast(I32).rearrange("f s (q r) n -> r q (f s) n", r=4)
             for r in range(4):
-                nc.sync.dma_start(t[:].bitcast(I32)[r:P:32, :, :], rows[r])
+                queue.dma_start(t[:].bitcast(I32)[r:P:32, :, :], rows[r])
 
         offsets = held.tile([P, E * C // 16], U16, name="offsets")
         xs = held.tile([P, PASSES, T], U8, name="xs", align_bytes=64)
-        nc.gpsimd.memset(xs[:].rearrange("p a n -> p (a n)").bitcast(I32), 0)
-        s1_early = zeroed("s1_early", 3 * PASSES, H)
-        s3_early = zeroed("s3_early", 3 * PASSES, H)
+        nc.vector.memset(xs[:].rearrange("p a n -> p (a n)").bitcast(I32), 0)
+        s1_early = held.tile([P, 3 * PASSES, H], U8, name="s1_early", align_bytes=64)
+        s3_early = held.tile([P, 3 * PASSES, H], U8, name="s3_early", align_bytes=64)
+        ident = held.tile([P, P], F32, name="ident")
+        make_identity(nc, ident[:])
+        s1_late = held.tile([P, 2 * PASSES, H], U8, name="s1_late", align_bytes=64)
+        s3_late = held.tile([P, 2 * PASSES, H], U8, name="s3_late", align_bytes=64)
+        load_rows(s1_late, w1c_scales[0:2], nc.gpsimd)
+        load_rows(s3_late, w3c_scales[0:2], nc.gpsimd)
         token_rows = x_scales.bitcast(I32).rearrange("s (q r) n -> r q s n", r=4)
         xw = held.tile([P, PASSES, T], I32, name="xw", align_bytes=64)
 
@@ -79,8 +80,6 @@ def tile_moe_hot_s_glu_sigmoid_kernel(
         load_cold(w1, w1c_words, 5, 6)
         load_cold(w3, w3c_words, 5, 6)
 
-        ident = held.tile([P, P], F32, name="ident")
-        make_identity(nc, ident[:])
         ysb = held.tile([P, E * C], F32, name="ysb")
 
         gw = held.tile([P, PASSES, E * C], U32, name="gw", align_bytes=64)
@@ -192,17 +191,10 @@ def tile_moe_hot_s_glu_sigmoid_kernel(
 
         hs = {i: hidden(i) for i in range(AHEAD)}
 
-        def spent(matrix, i, rows, width):
-            return held.tile([P, rows, width], U8, name="w%d_%d" % (matrix, ORDER[i]), align_bytes=64)
-
-        s1_late = spent(1, 0, 2 * PASSES, H)
-        s3_late = spent(3, 0, 2 * PASSES, H)
-        s1_hot = spent(1, 1, PASSES, H)
-        s3_hot = spent(3, 1, PASSES, H)
-        s2c = spent(1, 2, COLD, N)
-        s2h = spent(3, 2, 1, N)
-        load_rows(s1_late, w1c_scales[0:2])
-        load_rows(s3_late, w3c_scales[0:2])
+        s1_hot = held.tile([P, PASSES, H], U8, name="s1_hot", align_bytes=64)
+        s3_hot = held.tile([P, PASSES, H], U8, name="s3_hot", align_bytes=64)
+        s2c = held.tile([P, COLD, N], U8, name="s2c", align_bytes=64)
+        s2h = held.tile([P, 1, N], U8, name="s2h", align_bytes=64)
         load_cold(w1, w1c_words, 1, 2)
         load_cold(w3, w3c_words, 1, 2)
         load_rows(s1_hot, w1h_scales)

@@ -20,8 +20,9 @@ FP4X4 = mybir.dt.float4_e2m1fn_x4
 SIGMOID = mybir.ActivationFunctionType.Sigmoid
 MULT = mybir.AluOpType.mult
 
-ORDER = [3, 4, 5, 1, 2, 0]
-AHEAD = 3
+ORDER = list(range(E - 1, -1, -1))
+LATE_SLOTS = 2
+LATE_ROWS = 3
 
 
 def tile_moe_hot_s_glu_sigmoid_kernel(
@@ -34,88 +35,102 @@ def tile_moe_hot_s_glu_sigmoid_kernel(
         ring = ctx.enter_context(tc.tile_pool(name="ring", bufs=3))
         psum = ctx.enter_context(tc.psum_pool(name="psum", bufs=1))
 
-        def load_rows(t, scales, queue=nc.sync):
-            rows = scales.bitcast(I32).rearrange("f s (q r) n -> r q (f s) n", r=4)
+        def load_plane(name, scales, queue):
+            count, passes, rows, width = scales.shape
+            plane = held.tile([P, count * passes, width], U8, name=name, align_bytes=64)
+            by_row = scales.bitcast(I32).rearrange("f s (q r) n -> r q (f s) n", r=4)
             for r in range(4):
-                queue.dma_start(t[:].bitcast(I32)[r:P:32, :, :], rows[r])
+                queue.dma_start(plane[:].bitcast(I32)[r:P:32, :, :], by_row[r])
+            return plane
+
+        w1, w3, w2, s1, s3 = {}, {}, {}, {}, {}
+
+        def load_cold_rows(into, name, scales, first, end, queue):
+            plane = load_plane(name, scales[first - 1 : end - 1], queue)
+            for e in range(first, end):
+                into[e] = [plane[:, (e - first) * PASSES + s, :] for s in range(PASSES)]
+
+        def load_cold_words(into, name, words, e):
+            t = held.tile([P, PASSES, 2 * H], U8, name="%s_%d" % (name, e), align_bytes=64)
+            nc.sync.dma_start(t[:].bitcast(I32), words[e - 1].bitcast(I32).rearrange("s p n -> p s n"))
+            into[e] = [t[:, s, :].bitcast(FP4X4) for s in range(PASSES)]
+
+        load_cold_rows(s3, "s3c", w3c_scales, 1, E, nc.gpsimd)
 
         offsets = held.tile([P, E * C // 16], U16, name="offsets")
         xs = held.tile([P, PASSES, T], U8, name="xs", align_bytes=64)
-        nc.vector.memset(xs[:].rearrange("p a n -> p (a n)").bitcast(I32), 0)
-        s1_early = held.tile([P, 3 * PASSES, H], U8, name="s1_early", align_bytes=64)
-        s3_early = held.tile([P, 3 * PASSES, H], U8, name="s3_early", align_bytes=64)
-        ident = held.tile([P, P], F32, name="ident")
-        make_identity(nc, ident[:])
-        s1_late = held.tile([P, 2 * PASSES, H], U8, name="s1_late", align_bytes=64)
-        s3_late = held.tile([P, 2 * PASSES, H], U8, name="s3_late", align_bytes=64)
-        load_rows(s1_late, w1c_scales[0:2], nc.gpsimd)
-        load_rows(s3_late, w3c_scales[0:2], nc.gpsimd)
-        token_rows = x_scales.bitcast(I32).rearrange("s (q r) n -> r q s n", r=4)
+        xs_words = xs[:].rearrange("p a n -> p (a n)").bitcast(I32)
+        cut = PASSES * T // 8 - 1
+        nc.vector.memset(xs_words[:, :cut], 0)
+        nc.vector.memset(xs_words[:, cut:], 0)
         xw = held.tile([P, PASSES, T], I32, name="xw", align_bytes=64)
 
-        w1, w3, w2 = {}, {}, {}
-
-        def load_cold(into, words, first, end):
-            t = held.tile([P, (end - first) * PASSES, 2 * H], U8, name="w%d_%d" % (1 if into is w1 else 3, first), align_bytes=64)
-            nc.sync.dma_start(t[:].bitcast(I32), words[first - 1 : end - 1].bitcast(I32).rearrange("f s p n -> p (f s) n"))
-            for e in range(first, end):
-                into[e] = [t[:, (e - first) * PASSES + s, :].bitcast(FP4X4) for s in range(PASSES)]
-
-        def load_second(first, end):
-            t = held.tile([P, end - first, 2 * N], U8, name="w2c%d" % first, align_bytes=64)
-            nc.sync.dma_start(t[:].bitcast(I32), w2c_words[first - 1 : end - 1].bitcast(I32).rearrange("f s p n -> p (f s) n"))
-            for e in range(first, end):
-                w2[e] = t[:, e - first, :].bitcast(FP4X4)
-
-        load_cold(w1, w1c_words, 3, 4)
+        load_cold_words(w1, "w1", w1c_words, ORDER[0])
         nc.sync.dma_start(offsets[:], offs)
+        token_rows = x_scales.bitcast(I32).rearrange("s (q r) n -> r q s n", r=4)
         for r in range(4):
             nc.sync.dma_start(xs[:].bitcast(I32)[r:P:32, :, :], token_rows[r])
         nc.sync.dma_start(xw[:], x_words.rearrange("s p t d -> p s (t d)").bitcast(I32))
-        load_rows(s1_early, w1c_scales[2:5])
-        load_rows(s3_early, w3c_scales[2:5])
-        load_cold(w3, w3c_words, 3, 4)
-        load_cold(w1, w1c_words, 4, 5)
-        load_cold(w3, w3c_words, 4, 5)
-        load_cold(w1, w1c_words, 5, 6)
-        load_cold(w3, w3c_words, 5, 6)
+        load_cold_rows(s1, "s1c_early", w1c_scales, LATE_ROWS, E, nc.sync)
+        load_cold_words(w3, "w3", w3c_words, ORDER[0])
+        for e in range(E - 2, LATE_ROWS - 1, -1):
+            load_cold_words(w1, "w1", w1c_words, e)
+            load_cold_words(w3, "w3", w3c_words, e)
+        load_cold_rows(s1, "s1c_late", w1c_scales, 1, LATE_ROWS, nc.sync)
+        load_cold_words(w1, "w1", w1c_words, 2)
+        load_cold_words(w3, "w3", w3c_words, 2)
+        s1h = load_plane("s1h", w1h_scales, nc.sync)
+        load_cold_words(w1, "w1", w1c_words, 1)
+        load_cold_words(w3, "w3", w3c_words, 1)
+        s3h = load_plane("s3h", w3h_scales, nc.sync)
+        w1h = held.tile([P, PASSES, 4 * H], U8, name="w1h", align_bytes=64)
+        nc.sync.dma_start(w1h[:].bitcast(I32), w1h_words[0].rearrange("s p n d -> p s (n d)").bitcast(I32))
+        w1[0] = [w1h[:, s, :].bitcast(FP8X4) for s in range(PASSES)]
+        s1[0] = [s1h[:, s, :] for s in range(PASSES)]
+        hot3 = {}
+        for s in range(PASSES):
+            src = w3h_words[0, s].rearrange("p n d -> p (n d)").bitcast(I32)
+            for first, end in [(0, 2)] if s < PASSES - 1 else [(0, 1), (1, 2)]:
+                t = held.tile([P, (end - first) * 2 * H], U8, name="w3h_%d_%d" % (s, first), align_bytes=64)
+                nc.sync.dma_start(t[:].bitcast(I32), src[:, first * H // 2 : end * H // 2])
+                for u in range(first, end):
+                    hot3[(s, u)] = t[:, (u - first) * 2 * H : (u - first + 1) * 2 * H].bitcast(FP8X4)
+        w2c = held.tile([P, COLD, 2 * N], U8, name="w2c", align_bytes=64)
+        nc.sync.dma_start(w2c[:].bitcast(I32), w2c_words.bitcast(I32).rearrange("f s p n -> p (f s) n"))
+        s2c = load_plane("s2c", w2c_scales, nc.sync)
+        w2h = held.tile([P, 4 * N], U8, name="w2h", align_bytes=64)
+        nc.sync.dma_start(w2h[:].bitcast(I32), w2h_words[0, 0].rearrange("p n d -> p (n d)").bitcast(I32))
+        s2h = load_plane("s2h", w2h_scales, nc.sync)
+        for e in range(1, E):
+            w2[e] = (w2c[:, e - 1, :].bitcast(FP4X4), s2c[:, e - 1, :])
+        w2[0] = (w2h[:].bitcast(FP8X4), s2h[:, 0, :])
 
+        ident = held.tile([P, P], F32, name="ident")
+        nc.vector.memset(ident[:], 0.0)
+        make_identity(nc, ident[:], nomemset=True)
         ysb = held.tile([P, E * C], F32, name="ysb")
 
-        gw = held.tile([P, PASSES, E * C], U32, name="gw", align_bytes=64)
-        gs = held.tile([P, PASSES, AHEAD * C], U8, name="gs", align_bytes=64)
+        slot_words, slot_bytes = {}, {}
 
-        def entries(first, end):
-            return offsets[:, first * C // 16 : end * C // 16]
-
-        def gather_words(first, end):
+        def gather(into, window, dtype, name, first, end):
+            t = held.tile([P, PASSES, (end - first) * C], dtype, name=name, align_bytes=64)
+            entries = offsets[:, first * C // 16 : end * C // 16]
             for s in range(PASSES):
-                nc.vector.tensor_copy(gw[:, s, first * C : end * C], xw[:, s, :].bitcast(U32).indirect(entries(first, end)))
+                nc.vector.tensor_copy(t[:, s, :], window[:, s, :].indirect(entries))
+            for e in range(first, end):
+                into[e] = [t[:, s, (e - first) * C : (e - first + 1) * C] for s in range(PASSES)]
 
-        def gather_scales(into, first, end):
-            for s in range(PASSES):
-                nc.vector.tensor_copy(into[:, s, :], xs[:, s, :].indirect(entries(first, end)))
-
-        gather_scales(gs, AHEAD, E)
-        gather_words(AHEAD, AHEAD + 1)
-        gather_words(AHEAD + 1, E)
-        gather_words(0, AHEAD)
-        gs_late = held.tile([P, PASSES, AHEAD * C], U8, name="xw", align_bytes=64)
-        gather_scales(gs_late, 0, AHEAD)
-
-        def cold_rows(matrix, e):
-            if e >= 3:
-                t, place = (s1_early if matrix == 1 else s3_early), e - 3
-            else:
-                t, place = (s1_late if matrix == 1 else s3_late), e - 1
-            return [t[:, place * PASSES + s, :] for s in range(PASSES)]
+        xw_words = xw[:].bitcast(U32)
+        gather(slot_bytes, xs, U8, "bytes_early", LATE_SLOTS, E)
+        gather(slot_words, xw_words, U32, "words_first", E - 1, E)
+        gather(slot_words, xw_words, U32, "words_early", LATE_SLOTS, E - 1)
 
         def first_layer(e, words, scales, acc):
             for s in range(PASSES):
                 nc.tensor.matmul_mx(
                     out=acc,
-                    lhsT=gw[:, s, e * C : (e + 1) * C].bitcast(FP8X4),
-                    lhsT_scale=(gs if e >= AHEAD else gs_late)[:, s, e % AHEAD * C : (e % AHEAD + 1) * C],
+                    lhsT=slot_words[e][s].bitcast(FP8X4),
+                    lhsT_scale=slot_bytes[e][s],
                     rhs=words[s],
                     rhs_scale=scales[s],
                     start=(s == 0),
@@ -125,41 +140,42 @@ def tile_moe_hot_s_glu_sigmoid_kernel(
         def paired(acc):
             return acc.rearrange("j (p u v) -> j u p v", u=2, v=2)
 
-        gate_banks = [psum.tile([P, H], F32, name="gate_bank%d" % j) for j in range(3)]
-        lin_banks = [psum.tile([P, H], F32, name="lin_bank%d" % j) for j in range(3)]
-        spare = [psum.tile([P, H], F32, name="spare%d" % j) for j in range(2)]
+        gate_banks = [psum.tile([P, H], F32, name="gate_bank%d" % j) for j in range(2)]
+        lin_banks = [[psum.tile([P, H], F32, name="lin_bank%d_%d" % (u, j)) for j in range(2)] for u in range(2)]
+        result_banks = [psum.tile([P, H], F32, name="result_bank%d" % j) for j in range(2)]
+
+        def result_in(e):
+            if e >= 2:
+                return result_banks[0][:, (e - 2) * C : (e - 1) * C]
+            return (result_banks[1] if e else gate_banks[1])[:, :C]
+
+        def halves(e, u):
+            if e:
+                cols = slice(u * H // 2, (u + 1) * H // 2)
+                return [w[:, cols] for w in w3[e]], [z[:, cols] for z in s3[e]]
+            return [hot3[(s, u)] for s in range(PASSES)], [s3h[:, s, u * H // 2 : (u + 1) * H // 2] for s in range(PASSES)]
+
+        def products(i):
+            e = ORDER[i]
+            a = gate_banks[i % 2]
+            first_layer(e, w1[e], s1[e], a[:])
+            gate = ring.tile([P, 2, P, 2], F32, name="gate")
+            nc.scalar.activation(gate[:], paired(a[:]), SIGMOID)
+            for u in range(2):
+                first_layer(e, *halves(e, u), lin_banks[u][i % 2][:, : H // 2])
+            return gate
+
+        def hidden(i, gate):
+            h = ring.tile([P, 2, P, 2], BF16, name="h", align_bytes=64)
+            for u in range(2):
+                rows = slice(u * P // 2, (u + 1) * P // 2)
+                nc.vector.tensor_tensor(h[:, :, rows, :], paired(lin_banks[u][i % 2][:, : H // 2]), gate[:, :, rows, :], MULT)
+            return h
 
         def turned_in(i):
             if i < E - 2:
-                return gate_banks[(i | 1) + 1 - 3 * (i // 2)][:, i % 2 * 2 * C : (i % 2 + 1) * 2 * C]
-            return (spare[0] if i == E - 2 else gate_banks[0])[:, 0 : 2 * C]
-
-        def result_in(i):
-            e = ORDER[i]
-            if e >= 2:
-                return spare[1][:, (e - 2) * C : (e - 1) * C]
-            return (lin_banks[1] if e else spare[0])[:, 2 * C : 3 * C]
-
-        def hidden(i):
-            e = ORDER[i]
-            a = gate_banks[i % 3]
-            passes = range(PASSES)
-            first_layer(e, w1[e], cold_rows(1, e) if e else [s1_hot[:, s, :] for s in passes], a[:])
-            gate = ring.tile([P, 2, P, 2], F32, name="gate")
-            nc.scalar.activation(gate[:], paired(a[:]), SIGMOID)
-            h = ring.tile([P, 2, P, 2], BF16, name="h", align_bytes=64)
-            if e:
-                b = lin_banks[i % 3]
-                first_layer(e, w3[e], cold_rows(3, e), b[:])
-                nc.vector.tensor_tensor(h[:], paired(b[:]), gate[:], MULT)
-                return h
-            for u in range(2):
-                b = lin_banks[(i + u) % 3][:, 0 : H // 2]
-                cols = slice(u * H // 2, (u + 1) * H // 2)
-                first_layer(e, [hot3[(s, u)] for s in passes], [s3_hot[:, s, cols] for s in passes], b)
-                rows = slice(u * P // 2, (u + 1) * P // 2)
-                nc.vector.tensor_tensor(h[:, :, rows, :], paired(b), gate[:, :, rows, :], MULT)
-            return h
+                return lin_banks[1][(i + 1) % 2][:, H // 2 :]
+            return (gate_banks[0] if i == E - 2 else lin_banks[0][0])[:, H // 2 :]
 
         def turn(i, h):
             pairs = h[:].rearrange("j u p v -> j (u p v)").bitcast(F32)
@@ -177,63 +193,38 @@ def tile_moe_hot_s_glu_sigmoid_kernel(
             nc.vector.quantize_mx(out=codes[:].bitcast(FP8X4), scales=scales[:], in_=ht[:])
             return codes, scales
 
-        def second_layer(i, codes, scales):
-            e = ORDER[i]
+        def second_layer(e, codes, scales):
             nc.tensor.matmul_mx(
-                out=result_in(i),
-                lhsT=w2[e],
-                lhsT_scale=s2c[:, e - 1, :] if e else s2h[:, 0, :],
+                out=result_in(e),
+                lhsT=w2[e][0],
+                lhsT_scale=w2[e][1],
                 rhs=codes[:].bitcast(FP8X4),
                 rhs_scale=scales[:],
                 start=True,
                 stop=True,
             )
 
-        hs = {i: hidden(i) for i in range(AHEAD)}
-
-        s1_hot = held.tile([P, PASSES, H], U8, name="s1_hot", align_bytes=64)
-        s3_hot = held.tile([P, PASSES, H], U8, name="s3_hot", align_bytes=64)
-        s2c = held.tile([P, COLD, N], U8, name="s2c", align_bytes=64)
-        s2h = held.tile([P, 1, N], U8, name="s2h", align_bytes=64)
-        load_cold(w1, w1c_words, 1, 2)
-        load_cold(w3, w3c_words, 1, 2)
-        load_rows(s1_hot, w1h_scales)
-        load_cold(w1, w1c_words, 2, 3)
-        load_cold(w3, w3c_words, 2, 3)
-        load_rows(s3_hot, w3h_scales)
-        w1h = held.tile([P, PASSES, 4 * H], U8, name="w1h", align_bytes=64)
-        nc.sync.dma_start(w1h[:].bitcast(I32), w1h_words[0].rearrange("s p n d -> p s (n d)").bitcast(I32))
-        w1[0] = [w1h[:, s, :].bitcast(FP8X4) for s in range(PASSES)]
-        hot3 = {}
-        for s in range(PASSES):
-            src = w3h_words[0, s].rearrange("p n d -> p (n d)").bitcast(I32)
-            for first, end in [(0, 2)] if s < PASSES - 1 else [(0, 1), (1, 2)]:
-                t = held.tile([P, (end - first) * 2 * H], U8, name="w3h_%d_%d" % (s, first), align_bytes=64)
-                nc.sync.dma_start(t[:].bitcast(I32), src[:, first * H // 2 : end * H // 2])
-                for u in range(first, end):
-                    hot3[(s, u)] = t[:, (u - first) * 2 * H : (u - first + 1) * 2 * H].bitcast(FP8X4)
-        load_second(1, E)
-        load_rows(s2c, w2c_scales)
-        w2h = held.tile([P, 4 * N], U8, name="w2h", align_bytes=64)
-        nc.sync.dma_start(w2h[:].bitcast(I32), w2h_words[0, 0].rearrange("p n d -> p (n d)").bitcast(I32))
-        w2[0] = w2h[:].bitcast(FP8X4)
-        load_rows(s2h, w2h_scales)
-
-        quantised = {}
-        for i in range(E + 1):
-            if AHEAD <= i < E:
-                hs[i] = hidden(i)
-            ready = {2: [0, 1], 4: [2, 3], 5: [4], 6: [5]}.get(i, [])
-            for j in ready:
-                turn(j, hs[j])
-            for j in ready:
-                quantised[j] = quantise(j)
+        hs, quantised = {}, {}
+        for i in range(E):
+            gate = products(i)
+            if 0 < i < E - 1:
+                turn(i - 1, hs[i - 1])
+            hs[i] = hidden(i, gate)
+            if i == 0:
+                gather(slot_words, xw_words, U32, "w1_%d" % ORDER[0], 0, LATE_SLOTS)
+            if i == 1:
+                gather(slot_bytes, xs, U8, "w3_%d" % ORDER[1], 0, LATE_SLOTS)
+            if 0 < i < E - 1:
+                quantised[ORDER[i - 1]] = quantise(i - 1)
+            if i >= E - 2:
+                turn(i, hs[i])
+                quantised[ORDER[i]] = quantise(i)
         for e in range(COLD, 0, -1):
-            second_layer(ORDER.index(e), *quantised[ORDER.index(e)])
-        nc.scalar.copy(ysb[:, 2 * C :], spare[1][:])
+            second_layer(e, *quantised[e])
+        nc.scalar.copy(ysb[:, 2 * C :], result_banks[0][:])
         nc.sync.dma_start(out[:, 2 * C :], ysb[:, 2 * C :])
-        second_layer(COLD, *quantised[COLD])
-        nc.vector.tensor_copy(ysb[:, C : 2 * C], result_in(ORDER.index(1)))
+        second_layer(0, *quantised[0])
+        nc.vector.tensor_copy(ysb[:, C : 2 * C], result_in(1))
         nc.sync.dma_start(out[:, C : 2 * C], ysb[:, C : 2 * C])
-        nc.scalar.copy(ysb[:, :C], result_in(COLD))
+        nc.scalar.copy(ysb[:, :C], result_in(0))
         nc.sync.dma_start(out[:, :C], ysb[:, :C])

@@ -1,7 +1,6 @@
 from contextlib import ExitStack
 
 import concourse.mybir as mybir
-from concourse.masks import make_identity
 
 K, T, E, C, H, N = 1536, 768, 6, 128, 512, 128
 P = 128
@@ -23,6 +22,7 @@ MULT = mybir.AluOpType.mult
 ORDER = list(range(E - 1, -1, -1))
 LATE_SLOTS = 2
 LATE_ROWS = 3
+EARLY_BYTES = PASSES * (E - LATE_SLOTS) * C
 
 
 def tile_moe_hot_s_glu_sigmoid_kernel(
@@ -33,6 +33,7 @@ def tile_moe_hot_s_glu_sigmoid_kernel(
     with ExitStack() as ctx:
         held = ctx.enter_context(tc.tile_pool(name="held", bufs=1))
         ring = ctx.enter_context(tc.tile_pool(name="ring", bufs=3))
+        early = ctx.enter_context(tc.tile_pool(name="early", bufs=1))
         psum = ctx.enter_context(tc.psum_pool(name="psum", bufs=1))
 
         def load_plane(name, scales, queue):
@@ -57,6 +58,9 @@ def tile_moe_hot_s_glu_sigmoid_kernel(
 
         load_cold_rows(s3, "s3c", w3c_scales, 1, E, nc.gpsimd)
 
+        diagonal = early.tile([P, P], I32, name="diagonal", align_bytes=64, offset=EARLY_BYTES - 2 * P)
+        nc.gpsimd.iota(diagonal[:], [[1, P]], base=0, channel_multiplier=-1)
+
         offsets = held.tile([P, E * C // 16], U16, name="offsets")
         xs = held.tile([P, PASSES, T], U8, name="xs", align_bytes=64)
         xs_words = xs[:].rearrange("p a n -> p (a n)").bitcast(I32)
@@ -64,6 +68,8 @@ def tile_moe_hot_s_glu_sigmoid_kernel(
         nc.vector.memset(xs_words[:, :cut], 0)
         nc.vector.memset(xs_words[:, cut:], 0)
         xw = held.tile([P, PASSES, T], I32, name="xw", align_bytes=64)
+        ident = held.tile([P, P], F32, name="ident")
+        nc.vector.tensor_single_scalar(ident[:], diagonal[:], 0, mybir.AluOpType.is_equal)
 
         load_cold_words(w1, "w1", w1c_words, ORDER[0])
         nc.sync.dma_start(offsets[:], offs)
@@ -105,25 +111,28 @@ def tile_moe_hot_s_glu_sigmoid_kernel(
             w2[e] = (w2c[:, e - 1, :].bitcast(FP4X4), s2c[:, e - 1, :])
         w2[0] = (w2h[:].bitcast(FP8X4), s2h[:, 0, :])
 
-        ident = held.tile([P, P], F32, name="ident")
-        nc.vector.memset(ident[:], 0.0)
-        make_identity(nc, ident[:], nomemset=True)
         ysb = held.tile([P, E * C], F32, name="ysb")
 
         slot_words, slot_bytes = {}, {}
 
-        def gather(into, window, dtype, name, first, end):
-            t = held.tile([P, PASSES, (end - first) * C], dtype, name=name, align_bytes=64)
+        def gather_into(t, into, window, first, end):
             entries = offsets[:, first * C // 16 : end * C // 16]
             for s in range(PASSES):
                 nc.vector.tensor_copy(t[:, s, :], window[:, s, :].indirect(entries))
             for e in range(first, end):
                 into[e] = [t[:, s, (e - first) * C : (e - first + 1) * C] for s in range(PASSES)]
 
+        def gather(into, window, dtype, name, first, end):
+            t = held.tile([P, PASSES, (end - first) * C], dtype, name=name, align_bytes=64)
+            gather_into(t[:], into, window, first, end)
+
         xw_words = xw[:].bitcast(U32)
-        gather(slot_bytes, xs, U8, "bytes_early", LATE_SLOTS, E)
-        gather(slot_words, xw_words, U32, "words_first", E - 1, E)
-        gather(slot_words, xw_words, U32, "words_early", LATE_SLOTS, E - 1)
+        bytes_early = early.tile([P, PASSES, (E - LATE_SLOTS) * C], U8, name="bytes_early", align_bytes=64, offset=0)
+        words_early = early.tile([P, PASSES, (E - LATE_SLOTS) * C], U32, name="words_early", align_bytes=64, offset=EARLY_BYTES)
+        gather_into(bytes_early[:, :, 2 * C :], slot_bytes, xs, E - 2, E)
+        gather_into(words_early[:, :, (E - LATE_SLOTS - 1) * C :], slot_words, xw_words, E - 1, E)
+        gather_into(words_early[:, :, : (E - LATE_SLOTS - 1) * C], slot_words, xw_words, LATE_SLOTS, E - 1)
+        gather_into(bytes_early[:, :, : 2 * C], slot_bytes, xs, LATE_SLOTS, E - 2)
 
         def first_layer(e, words, scales, acc):
             for s in range(PASSES):
@@ -140,42 +149,46 @@ def tile_moe_hot_s_glu_sigmoid_kernel(
         def paired(acc):
             return acc.rearrange("j (p u v) -> j u p v", u=2, v=2)
 
-        gate_banks = [psum.tile([P, H], F32, name="gate_bank%d" % j) for j in range(2)]
-        lin_banks = [[psum.tile([P, H], F32, name="lin_bank%d_%d" % (u, j)) for j in range(2)] for u in range(2)]
-        result_banks = [psum.tile([P, H], F32, name="result_bank%d" % j) for j in range(2)]
+        gate_banks = [[psum.tile([P, H], F32, name="gate_bank%d_%d" % (u, j)) for j in range(2)] for u in range(2)]
+        lin_banks = [psum.tile([P, H], F32, name="lin_bank%d" % j) for j in range(3)]
+        result_bank = psum.tile([P, H], F32, name="result_bank")
+        HALF = H // 2
 
         def result_in(e):
             if e >= 2:
-                return result_banks[0][:, (e - 2) * C : (e - 1) * C]
-            return (result_banks[1] if e else gate_banks[1])[:, :C]
+                return result_bank[:, (e - 2) * C : (e - 1) * C]
+            return (gate_banks[1][0] if e else gate_banks[0][1])[:, :C]
 
-        def halves(e, u):
-            if e:
-                cols = slice(u * H // 2, (u + 1) * H // 2)
-                return [w[:, cols] for w in w3[e]], [z[:, cols] for z in s3[e]]
-            return [hot3[(s, u)] for s in range(PASSES)], [s3h[:, s, u * H // 2 : (u + 1) * H // 2] for s in range(PASSES)]
-
-        def products(i):
+        def gate_products(i):
             e = ORDER[i]
-            a = gate_banks[i % 2]
-            first_layer(e, w1[e], s1[e], a[:])
-            gate = ring.tile([P, 2, P, 2], F32, name="gate")
-            nc.scalar.activation(gate[:], paired(a[:]), SIGMOID)
             for u in range(2):
-                first_layer(e, *halves(e, u), lin_banks[u][i % 2][:, : H // 2])
-            return gate
+                cols = slice(u * HALF, (u + 1) * HALF)
+                first_layer(e, [w[:, cols] for w in w1[e]], [z[:, cols] for z in s1[e]], gate_banks[u][i % 2][:, :HALF])
 
-        def hidden(i, gate):
-            h = ring.tile([P, 2, P, 2], BF16, name="h", align_bytes=64)
+        def hidden(i):
+            e = ORDER[i]
+            gate = ring.tile([P, 2, P, 2], F32, name="gate")
             for u in range(2):
                 rows = slice(u * P // 2, (u + 1) * P // 2)
-                nc.vector.tensor_tensor(h[:, :, rows, :], paired(lin_banks[u][i % 2][:, : H // 2]), gate[:, :, rows, :], MULT)
+                nc.scalar.activation(gate[:, :, rows, :], paired(gate_banks[u][i % 2][:, :HALF]), SIGMOID)
+            h = ring.tile([P, 2, P, 2], BF16, name="h", align_bytes=64)
+            if e:
+                first_layer(e, w3[e], s3[e], lin_banks[i % 3][:])
+                nc.vector.tensor_tensor(h[:], paired(lin_banks[i % 3][:]), gate[:], MULT)
+                return h
+            for u in range(2):
+                b = lin_banks[(i + u) % 3][:, :HALF]
+                first_layer(e, [hot3[(s, u)] for s in range(PASSES)], [s3h[:, s, u * HALF : (u + 1) * HALF] for s in range(PASSES)], b)
+                rows = slice(u * P // 2, (u + 1) * P // 2)
+                nc.vector.tensor_tensor(h[:, :, rows, :], paired(b), gate[:, :, rows, :], MULT)
             return h
 
         def turned_in(i):
-            if i < E - 2:
-                return lin_banks[1][(i + 1) % 2][:, H // 2 :]
-            return (gate_banks[0] if i == E - 2 else lin_banks[0][0])[:, H // 2 :]
+            if i < E - 3:
+                return gate_banks[1][i % 2][:, HALF:]
+            if i < E - 1:
+                return lin_banks[(E - 2) % 3][:, (E - 2 - i) * HALF : (E - 1 - i) * HALF]
+            return gate_banks[0][0][:, HALF:]
 
         def turn(i, h):
             pairs = h[:].rearrange("j u p v -> j (u p v)").bitcast(F32)
@@ -206,22 +219,24 @@ def tile_moe_hot_s_glu_sigmoid_kernel(
 
         hs, quantised = {}, {}
         for i in range(E):
-            gate = products(i)
-            if 0 < i < E - 1:
-                turn(i - 1, hs[i - 1])
-            hs[i] = hidden(i, gate)
+            gate_products(i)
+            if 2 <= i < E - 1:
+                turn(i - 2, hs[i - 2])
+            hs[i] = hidden(i)
             if i == 0:
-                gather(slot_words, xw_words, U32, "w1_%d" % ORDER[0], 0, LATE_SLOTS)
+                gather(slot_words, xw_words, U32, "w3_%d" % ORDER[0], 0, LATE_SLOTS)
             if i == 1:
                 gather(slot_bytes, xs, U8, "w3_%d" % ORDER[1], 0, LATE_SLOTS)
-            if 0 < i < E - 1:
-                quantised[ORDER[i - 1]] = quantise(i - 1)
-            if i >= E - 2:
-                turn(i, hs[i])
-                quantised[ORDER[i]] = quantise(i)
+            if 2 <= i < E - 1:
+                quantised[ORDER[i - 2]] = quantise(i - 2)
+            last = {E - 2: [E - 2, E - 3], E - 1: [E - 1]}.get(i, [])
+            for j in last:
+                turn(j, hs[j])
+            for j in last:
+                quantised[ORDER[j]] = quantise(j)
         for e in range(COLD, 0, -1):
             second_layer(e, *quantised[e])
-        nc.scalar.copy(ysb[:, 2 * C :], result_banks[0][:])
+        nc.scalar.copy(ysb[:, 2 * C :], result_bank[:])
         nc.sync.dma_start(out[:, 2 * C :], ysb[:, 2 * C :])
         second_layer(0, *quantised[0])
         nc.vector.tensor_copy(ysb[:, C : 2 * C], result_in(1))

@@ -22,7 +22,7 @@ MULT = mybir.AluOpType.mult
 ORDER = list(range(E - 1, -1, -1))
 LATE_SLOTS = 2
 LATE_ROWS = 3
-EARLY_BYTES = PASSES * (E - LATE_SLOTS) * C
+EARLY_BYTES = PASSES * 2 * C
 
 
 def tile_moe_hot_s_glu_sigmoid_kernel(
@@ -36,12 +36,15 @@ def tile_moe_hot_s_glu_sigmoid_kernel(
         early = ctx.enter_context(tc.tile_pool(name="early", bufs=1))
         psum = ctx.enter_context(tc.psum_pool(name="psum", bufs=1))
 
-        def load_plane(name, scales, queue):
-            count, passes, rows, width = scales.shape
-            plane = held.tile([P, count * passes, width], U8, name=name, align_bytes=64)
+        def load_rows(plane, scales, queue, rows):
             by_row = scales.bitcast(I32).rearrange("f s (q r) n -> r q (f s) n", r=4)
-            for r in range(4):
+            for r in rows:
                 queue.dma_start(plane[:].bitcast(I32)[r:P:32, :, :], by_row[r])
+
+        def load_plane(name, scales, queue, rows=range(4)):
+            count, passes, blocks, width = scales.shape
+            plane = held.tile([P, count * passes, width], U8, name=name, align_bytes=64)
+            load_rows(plane, scales, queue, rows)
             return plane
 
         w1, w3, w2, s1, s3 = {}, {}, {}, {}, {}
@@ -56,7 +59,9 @@ def tile_moe_hot_s_glu_sigmoid_kernel(
             nc.sync.dma_start(t[:].bitcast(I32), words[e - 1].bitcast(I32).rearrange("s p n -> p s n"))
             into[e] = [t[:, s, :].bitcast(FP4X4) for s in range(PASSES)]
 
-        load_cold_rows(s3, "s3c", w3c_scales, 1, E, nc.gpsimd)
+        s3c = load_plane("s3c", w3c_scales, nc.gpsimd, range(3))
+        for e in range(1, E):
+            s3[e] = [s3c[:, (e - 1) * PASSES + s, :] for s in range(PASSES)]
 
         diagonal = early.tile([P, P], I32, name="diagonal", align_bytes=64, offset=EARLY_BYTES - 2 * P)
         nc.gpsimd.iota(diagonal[:], [[1, P]], base=0, channel_multiplier=-1)
@@ -78,6 +83,7 @@ def tile_moe_hot_s_glu_sigmoid_kernel(
             nc.sync.dma_start(xs[:].bitcast(I32)[r:P:32, :, :], token_rows[r])
         nc.sync.dma_start(xw[:], x_words.rearrange("s p t d -> p s (t d)").bitcast(I32))
         load_cold_rows(s1, "s1c_early", w1c_scales, LATE_ROWS, E, nc.sync)
+        load_rows(s3c, w3c_scales, nc.sync, [3])
         load_cold_words(w3, "w3", w3c_words, ORDER[0])
         for e in range(E - 2, LATE_ROWS - 1, -1):
             load_cold_words(w1, "w1", w1c_words, e)
@@ -127,12 +133,11 @@ def tile_moe_hot_s_glu_sigmoid_kernel(
             gather_into(t[:], into, window, first, end)
 
         xw_words = xw[:].bitcast(U32)
-        bytes_early = early.tile([P, PASSES, (E - LATE_SLOTS) * C], U8, name="bytes_early", align_bytes=64, offset=0)
+        bytes_early = early.tile([P, PASSES, 2 * C], U8, name="bytes_early", align_bytes=64, offset=0)
         words_early = early.tile([P, PASSES, (E - LATE_SLOTS) * C], U32, name="words_early", align_bytes=64, offset=EARLY_BYTES)
-        gather_into(bytes_early[:, :, 2 * C :], slot_bytes, xs, E - 2, E)
+        gather_into(bytes_early[:], slot_bytes, xs, E - 2, E)
         gather_into(words_early[:, :, (E - LATE_SLOTS - 1) * C :], slot_words, xw_words, E - 1, E)
         gather_into(words_early[:, :, : (E - LATE_SLOTS - 1) * C], slot_words, xw_words, LATE_SLOTS, E - 1)
-        gather_into(bytes_early[:, :, : 2 * C], slot_bytes, xs, LATE_SLOTS, E - 2)
 
         def first_layer(e, words, scales, acc):
             for s in range(PASSES):
@@ -157,7 +162,7 @@ def tile_moe_hot_s_glu_sigmoid_kernel(
         def result_in(e):
             if e >= 2:
                 return result_bank[:, (e - 2) * C : (e - 1) * C]
-            return (gate_banks[1][0] if e else gate_banks[0][1])[:, :C]
+            return (lin_banks[1] if e else gate_banks[1][0])[:, :C]
 
         def gate_products(i):
             e = ORDER[i]
@@ -165,12 +170,15 @@ def tile_moe_hot_s_glu_sigmoid_kernel(
                 cols = slice(u * HALF, (u + 1) * HALF)
                 first_layer(e, [w[:, cols] for w in w1[e]], [z[:, cols] for z in s1[e]], gate_banks[u][i % 2][:, :HALF])
 
-        def hidden(i):
-            e = ORDER[i]
+        def gates(i):
             gate = ring.tile([P, 2, P, 2], F32, name="gate")
             for u in range(2):
                 rows = slice(u * P // 2, (u + 1) * P // 2)
                 nc.scalar.activation(gate[:, :, rows, :], paired(gate_banks[u][i % 2][:, :HALF]), SIGMOID)
+            return gate
+
+        def hidden(i, gate):
+            e = ORDER[i]
             h = ring.tile([P, 2, P, 2], BF16, name="h", align_bytes=64)
             if e:
                 first_layer(e, w3[e], s3[e], lin_banks[i % 3][:])
@@ -187,7 +195,7 @@ def tile_moe_hot_s_glu_sigmoid_kernel(
             if i < E - 3:
                 return gate_banks[1][i % 2][:, HALF:]
             if i < E - 1:
-                return lin_banks[(E - 2) % 3][:, (E - 2 - i) * HALF : (E - 1 - i) * HALF]
+                return gate_banks[i - (E - 3)][(E - 1) % 2][:, HALF:]
             return gate_banks[0][0][:, HALF:]
 
         def turn(i, h):
@@ -222,18 +230,21 @@ def tile_moe_hot_s_glu_sigmoid_kernel(
             gate_products(i)
             if 2 <= i < E - 1:
                 turn(i - 2, hs[i - 2])
-            hs[i] = hidden(i)
-            if i == 0:
-                gather(slot_words, xw_words, U32, "w3_%d" % ORDER[0], 0, LATE_SLOTS)
-            if i == 1:
-                gather(slot_bytes, xs, U8, "w3_%d" % ORDER[1], 0, LATE_SLOTS)
+            gate = gates(i)
+            if i < 2:
+                gather(slot_bytes, xs, U8, "w1_%d" % ORDER[i], 2 - 2 * i, 4 - 2 * i)
+            if i == E - 1:
+                for j in (E - 3, E - 2):
+                    turn(j, hs[j])
+                for j in (E - 3, E - 2):
+                    quantised[ORDER[j]] = quantise(j)
+            hs[i] = hidden(i, gate)
+            if i in (1, 2):
+                gather(slot_words, xw_words, U32, "w3_%d" % ORDER[i], 2 - i, 3 - i)
             if 2 <= i < E - 1:
                 quantised[ORDER[i - 2]] = quantise(i - 2)
-            last = {E - 2: [E - 2, E - 3], E - 1: [E - 1]}.get(i, [])
-            for j in last:
-                turn(j, hs[j])
-            for j in last:
-                quantised[ORDER[j]] = quantise(j)
+        turn(E - 1, hs[E - 1])
+        quantised[0] = quantise(E - 1)
         for e in range(COLD, 0, -1):
             second_layer(e, *quantised[e])
         nc.scalar.copy(ysb[:, 2 * C :], result_bank[:])

@@ -1,6 +1,7 @@
 from contextlib import ExitStack
 
 import concourse.mybir as mybir
+from concourse.masks import make_identity
 
 K, T, E, C, H, N = 1536, 768, 6, 128, 512, 128
 P = 128
@@ -22,7 +23,6 @@ MULT = mybir.AluOpType.mult
 ORDER = list(range(E - 1, -1, -1))
 LATE_SLOTS = 2
 LATE_ROWS = 3
-EARLY_BYTES = PASSES * 2 * C
 
 
 def tile_moe_hot_s_glu_sigmoid_kernel(
@@ -33,7 +33,6 @@ def tile_moe_hot_s_glu_sigmoid_kernel(
     with ExitStack() as ctx:
         held = ctx.enter_context(tc.tile_pool(name="held", bufs=1))
         ring = ctx.enter_context(tc.tile_pool(name="ring", bufs=3))
-        early = ctx.enter_context(tc.tile_pool(name="early", bufs=1))
         psum = ctx.enter_context(tc.psum_pool(name="psum", bufs=1))
 
         def load_rows(plane, scales, queue, rows):
@@ -59,22 +58,13 @@ def tile_moe_hot_s_glu_sigmoid_kernel(
             nc.sync.dma_start(t[:].bitcast(I32), words[e - 1].bitcast(I32).rearrange("s p n -> p s n"))
             into[e] = [t[:, s, :].bitcast(FP4X4) for s in range(PASSES)]
 
-        s3c = load_plane("s3c", w3c_scales, nc.gpsimd, range(3))
-        for e in range(1, E):
-            s3[e] = [s3c[:, (e - 1) * PASSES + s, :] for s in range(PASSES)]
-
-        diagonal = early.tile([P, P], I32, name="diagonal", align_bytes=64, offset=EARLY_BYTES - 2 * P)
-        nc.gpsimd.iota(diagonal[:], [[1, P]], base=0, channel_multiplier=-1)
 
         offsets = held.tile([P, E * C // 16], U16, name="offsets")
         xs = held.tile([P, PASSES, T], U8, name="xs", align_bytes=64)
-        xs_words = xs[:].rearrange("p a n -> p (a n)").bitcast(I32)
-        cut = PASSES * T // 8 - 1
-        nc.vector.memset(xs_words[:, :cut], 0)
-        nc.vector.memset(xs_words[:, cut:], 0)
+        nc.vector.memset(xs[:].rearrange("p a n -> p (a n)").bitcast(I32), 0)
         xw = held.tile([P, PASSES, T], I32, name="xw", align_bytes=64)
         ident = held.tile([P, P], F32, name="ident")
-        nc.vector.tensor_single_scalar(ident[:], diagonal[:], 0, mybir.AluOpType.is_equal)
+        make_identity(nc, ident[:])
 
         load_cold_words(w1, "w1", w1c_words, ORDER[0])
         nc.sync.dma_start(offsets[:], offs)
@@ -83,22 +73,26 @@ def tile_moe_hot_s_glu_sigmoid_kernel(
             nc.sync.dma_start(xs[:].bitcast(I32)[r:P:32, :, :], token_rows[r])
         nc.sync.dma_start(xw[:], x_words.rearrange("s p t d -> p s (t d)").bitcast(I32))
         load_cold_rows(s1, "s1c_early", w1c_scales, LATE_ROWS, E, nc.sync)
-        load_rows(s3c, w3c_scales, nc.sync, [3])
+        load_cold_rows(s3, "s3c_early", w3c_scales, LATE_ROWS, E, nc.sync)
         load_cold_words(w3, "w3", w3c_words, ORDER[0])
         for e in range(E - 2, LATE_ROWS - 1, -1):
             load_cold_words(w1, "w1", w1c_words, e)
             load_cold_words(w3, "w3", w3c_words, e)
         load_cold_rows(s1, "s1c_late", w1c_scales, 1, LATE_ROWS, nc.sync)
         load_cold_words(w1, "w1", w1c_words, 2)
+        load_cold_rows(s3, "s3c_late", w3c_scales, 1, LATE_ROWS, nc.sync)
         load_cold_words(w3, "w3", w3c_words, 2)
         s1h = load_plane("s1h", w1h_scales, nc.sync)
         load_cold_words(w1, "w1", w1c_words, 1)
         load_cold_words(w3, "w3", w3c_words, 1)
         s3h = load_plane("s3h", w3h_scales, nc.sync)
-        w1h = held.tile([P, PASSES, 4 * H], U8, name="w1h", align_bytes=64)
-        nc.sync.dma_start(w1h[:].bitcast(I32), w1h_words[0].rearrange("s p n d -> p s (n d)").bitcast(I32))
-        w1[0] = [w1h[:, s, :].bitcast(FP8X4) for s in range(PASSES)]
+        w1[0] = []
+        for s in range(PASSES):
+            t = held.tile([P, 4 * H], U8, name="w1h_%d" % s, align_bytes=64)
+            nc.sync.dma_start(t[:].bitcast(I32), w1h_words[0, s].rearrange("p n d -> p (n d)").bitcast(I32))
+            w1[0].append(t[:].bitcast(FP8X4))
         s1[0] = [s1h[:, s, :] for s in range(PASSES)]
+        s3[0] = [s3h[:, s, :] for s in range(PASSES)]
         hot3 = {}
         for s in range(PASSES):
             src = w3h_words[0, s].rearrange("p n d -> p (n d)").bitcast(I32)
@@ -133,70 +127,76 @@ def tile_moe_hot_s_glu_sigmoid_kernel(
             gather_into(t[:], into, window, first, end)
 
         xw_words = xw[:].bitcast(U32)
-        bytes_early = early.tile([P, PASSES, 2 * C], U8, name="bytes_early", align_bytes=64, offset=0)
-        words_early = early.tile([P, PASSES, (E - LATE_SLOTS) * C], U32, name="words_early", align_bytes=64, offset=EARLY_BYTES)
+        bytes_early = held.tile([P, PASSES, 2 * C], U8, name="bytes_early", align_bytes=64)
+        words_early = held.tile([P, PASSES, (E - LATE_SLOTS) * C], U32, name="words_early", align_bytes=64)
         gather_into(bytes_early[:], slot_bytes, xs, E - 2, E)
         gather_into(words_early[:, :, (E - LATE_SLOTS - 1) * C :], slot_words, xw_words, E - 1, E)
         gather_into(words_early[:, :, : (E - LATE_SLOTS - 1) * C], slot_words, xw_words, LATE_SLOTS, E - 1)
 
-        def first_layer(e, words, scales, acc):
+        def first_layer(e, parts):
             for s in range(PASSES):
-                nc.tensor.matmul_mx(
-                    out=acc,
-                    lhsT=slot_words[e][s].bitcast(FP8X4),
-                    lhsT_scale=slot_bytes[e][s],
-                    rhs=words[s],
-                    rhs_scale=scales[s],
-                    start=(s == 0),
-                    stop=(s == PASSES - 1),
-                )
+                for words, scales, acc in parts:
+                    nc.tensor.matmul_mx(
+                        out=acc,
+                        lhsT=slot_words[e][s].bitcast(FP8X4),
+                        lhsT_scale=slot_bytes[e][s],
+                        rhs=words[s],
+                        rhs_scale=scales[s],
+                        start=(s == 0),
+                        stop=(s == PASSES - 1),
+                    )
 
         def paired(acc):
             return acc.rearrange("j (p u v) -> j u p v", u=2, v=2)
 
-        gate_banks = [[psum.tile([P, H], F32, name="gate_bank%d_%d" % (u, j)) for j in range(2)] for u in range(2)]
-        lin_banks = [psum.tile([P, H], F32, name="lin_bank%d" % j) for j in range(3)]
-        result_bank = psum.tile([P, H], F32, name="result_bank")
+        gate_banks = [psum.tile([P, H], F32, name="gate_bank%d" % j) for j in range(2)]
+        lin_banks = [[psum.tile([P, H], F32, name="lin_bank%d_%d" % (j, u)) for u in range(2)] for j in range(2)]
+        result_banks = [psum.tile([P, H], F32, name="result_bank%d" % j) for j in range(2)]
         HALF = H // 2
 
         def result_in(e):
             if e >= 2:
-                return result_bank[:, (e - 2) * C : (e - 1) * C]
-            return (lin_banks[1] if e else gate_banks[1][0])[:, :C]
+                return result_banks[0][:, (e - 2) * C : (e - 1) * C]
+            return (result_banks[1] if e else gate_banks[1])[:, :C]
 
-        def gate_products(i):
-            e = ORDER[i]
-            for u in range(2):
-                cols = slice(u * HALF, (u + 1) * HALF)
-                first_layer(e, [w[:, cols] for w in w1[e]], [z[:, cols] for z in s1[e]], gate_banks[u][i % 2][:, :HALF])
+        def halved(tiles, u):
+            return [t[:, u * HALF : (u + 1) * HALF] for t in tiles]
+
+        def gate_sums(i):
+            if ORDER[i]:
+                return [gate_banks[i % 2][:]]
+            return [gate_banks[(i + u) % 2][:, :HALF] for u in range(2)]
+
+        def lin_sums(i):
+            if i < 2:
+                return [lin_banks[1][i][:]]
+            return [lin_banks[i % 2][u][:, :HALF] for u in range(2)]
+
+        def products(e, words, scales, sums):
+            if len(sums) == 1:
+                first_layer(e, [(words, scales, sums[0])])
+            else:
+                first_layer(e, [(halved(words, u), halved(scales, u), sums[u]) for u in range(2)])
+
+        def rows_of(sums, u):
+            return slice(u * P // len(sums), (u + 1) * P // len(sums))
 
         def gates(i):
             gate = ring.tile([P, 2, P, 2], F32, name="gate")
-            for u in range(2):
-                rows = slice(u * P // 2, (u + 1) * P // 2)
-                nc.scalar.activation(gate[:, :, rows, :], paired(gate_banks[u][i % 2][:, :HALF]), SIGMOID)
+            for u, acc in enumerate(gate_sums(i)):
+                nc.scalar.activation(gate[:, :, rows_of(gate_sums(i), u), :], paired(acc), SIGMOID)
             return gate
 
         def hidden(i, gate):
-            e = ORDER[i]
             h = ring.tile([P, 2, P, 2], BF16, name="h", align_bytes=64)
-            if e:
-                first_layer(e, w3[e], s3[e], lin_banks[i % 3][:])
-                nc.vector.tensor_tensor(h[:], paired(lin_banks[i % 3][:]), gate[:], MULT)
-                return h
-            for u in range(2):
-                b = lin_banks[(i + u) % 3][:, :HALF]
-                first_layer(e, [hot3[(s, u)] for s in range(PASSES)], [s3h[:, s, u * HALF : (u + 1) * HALF] for s in range(PASSES)], b)
-                rows = slice(u * P // 2, (u + 1) * P // 2)
-                nc.vector.tensor_tensor(h[:, :, rows, :], paired(b), gate[:, :, rows, :], MULT)
+            for u, acc in enumerate(lin_sums(i)):
+                rows = rows_of(lin_sums(i), u)
+                nc.vector.tensor_tensor(h[:, :, rows, :], paired(acc), gate[:, :, rows, :], MULT)
             return h
 
         def turned_in(i):
-            if i < E - 3:
-                return gate_banks[1][i % 2][:, HALF:]
-            if i < E - 1:
-                return gate_banks[i - (E - 3)][(E - 1) % 2][:, HALF:]
-            return gate_banks[0][0][:, HALF:]
+            banks = [lin_banks[0][0], lin_banks[0][1], lin_banks[1][1], lin_banks[0][1], gate_banks[0], lin_banks[0][0]]
+            return banks[i][:, HALF:]
 
         def turn(i, h):
             pairs = h[:].rearrange("j u p v -> j (u p v)").bitcast(F32)
@@ -226,28 +226,32 @@ def tile_moe_hot_s_glu_sigmoid_kernel(
             )
 
         hs, quantised = {}, {}
-        for i in range(E):
-            gate_products(i)
-            if 2 <= i < E - 1:
-                turn(i - 2, hs[i - 2])
+        for i, e in enumerate(ORDER):
+            products(e, w1[e], s1[e], gate_sums(i))
+            if not e:
+                turn(i - 1, hs[i - 1])
             gate = gates(i)
+            if not e:
+                quantised[ORDER[i - 1]] = quantise(i - 1)
             if i < 2:
-                gather(slot_bytes, xs, U8, "w1_%d" % ORDER[i], 2 - 2 * i, 4 - 2 * i)
-            if i == E - 1:
-                for j in (E - 3, E - 2):
-                    turn(j, hs[j])
-                for j in (E - 3, E - 2):
-                    quantised[ORDER[j]] = quantise(j)
+                gather(slot_bytes, xs, U8, "w1_%d" % e, 2 - 2 * i, 4 - 2 * i)
+            if e:
+                products(e, w3[e], s3[e], lin_sums(i))
+            else:
+                first_layer(e, [([hot3[(s, u)] for s in range(PASSES)], halved(s3[e], u), lin_sums(i)[u]) for u in range(2)])
+            behind = {2: [0, 1], 3: [2], 4: [3]}.get(i, [])
+            for j in behind:
+                turn(j, hs[j])
             hs[i] = hidden(i, gate)
             if i in (1, 2):
-                gather(slot_words, xw_words, U32, "w3_%d" % ORDER[i], 2 - i, 3 - i)
-            if 2 <= i < E - 1:
-                quantised[ORDER[i - 2]] = quantise(i - 2)
+                gather(slot_words, xw_words, U32, "w3_%d" % e, 2 - i, 3 - i)
+            for j in behind:
+                quantised[ORDER[j]] = quantise(j)
         turn(E - 1, hs[E - 1])
         quantised[0] = quantise(E - 1)
         for e in range(COLD, 0, -1):
             second_layer(e, *quantised[e])
-        nc.scalar.copy(ysb[:, 2 * C :], result_bank[:])
+        nc.scalar.copy(ysb[:, 2 * C :], result_banks[0][:])
         nc.sync.dma_start(out[:, 2 * C :], ysb[:, 2 * C :])
         second_layer(0, *quantised[0])
         nc.vector.tensor_copy(ysb[:, C : 2 * C], result_in(1))

@@ -73,24 +73,27 @@ def tile_moe_hot_s_glu_sigmoid_kernel(
             nc.sync.dma_start(xs[:].bitcast(I32)[r:P:32, :, :], token_rows[r])
         nc.sync.dma_start(xw[:], x_words.rearrange("s p t d -> p s (t d)").bitcast(I32))
         load_cold_rows(s1, "s1c_early", w1c_scales, LATE_ROWS, E, nc.sync)
-        load_cold_rows(s3, "s3c_early", w3c_scales, LATE_ROWS, E, nc.sync)
         load_cold_words(w3, "w3", w3c_words, ORDER[0])
-        for e in range(E - 2, LATE_ROWS - 1, -1):
+        load_cold_rows(s3, "s3c_early", w3c_scales, LATE_ROWS, E, nc.sync)
+        s2h = held.tile([P, 1, N], U8, name="s2h", align_bytes=64)
+        for i, e in enumerate(ORDER[1:COLD]):
             load_cold_words(w1, "w1", w1c_words, e)
+            if i < 3:
+                load_rows(s2h, w2h_scales, nc.sync, [i])
             load_cold_words(w3, "w3", w3c_words, e)
-        load_cold_rows(s1, "s1c_late", w1c_scales, 1, LATE_ROWS, nc.sync)
-        load_cold_words(w1, "w1", w1c_words, 2)
-        load_cold_rows(s3, "s3c_late", w3c_scales, 1, LATE_ROWS, nc.sync)
-        load_cold_words(w3, "w3", w3c_words, 2)
-        s1h = load_plane("s1h", w1h_scales, nc.sync)
-        load_cold_words(w1, "w1", w1c_words, 1)
-        load_cold_words(w3, "w3", w3c_words, 1)
-        s3h = load_plane("s3h", w3h_scales, nc.sync)
+            if i == 0:
+                load_cold_rows(s1, "s1c_late", w1c_scales, 1, LATE_ROWS, nc.sync)
+            if i == 1:
+                load_cold_rows(s3, "s3c_late", w3c_scales, 1, LATE_ROWS, nc.sync)
+            if i == 2:
+                s1h = load_plane("s1h", w1h_scales, nc.sync)
+            if i == 3:
+                s3h = load_plane("s3h", w3h_scales, nc.sync)
         w1[0] = []
-        for s in range(PASSES):
-            t = held.tile([P, 4 * H], U8, name="w1h_%d" % s, align_bytes=64)
-            nc.sync.dma_start(t[:].bitcast(I32), w1h_words[0, s].rearrange("p n d -> p (n d)").bitcast(I32))
-            w1[0].append(t[:].bitcast(FP8X4))
+        for first, end in ((0, PASSES - 1), (PASSES - 1, PASSES)):
+            t = held.tile([P, end - first, 4 * H], U8, name="w1h_%d" % first, align_bytes=64)
+            nc.sync.dma_start(t[:].bitcast(I32), w1h_words[0, first:end].rearrange("s p n d -> p s (n d)").bitcast(I32))
+            w1[0].extend(t[:, s, :].bitcast(FP8X4) for s in range(end - first))
         s1[0] = [s1h[:, s, :] for s in range(PASSES)]
         s3[0] = [s3h[:, s, :] for s in range(PASSES)]
         hot3 = {}
@@ -106,7 +109,7 @@ def tile_moe_hot_s_glu_sigmoid_kernel(
         s2c = load_plane("s2c", w2c_scales, nc.sync)
         w2h = held.tile([P, 4 * N], U8, name="w2h", align_bytes=64)
         nc.sync.dma_start(w2h[:].bitcast(I32), w2h_words[0, 0].rearrange("p n d -> p (n d)").bitcast(I32))
-        s2h = load_plane("s2h", w2h_scales, nc.sync)
+        load_rows(s2h, w2h_scales, nc.sync, [3])
         for e in range(1, E):
             w2[e] = (w2c[:, e - 1, :].bitcast(FP4X4), s2c[:, e - 1, :])
         w2[0] = (w2h[:].bitcast(FP8X4), s2h[:, 0, :])
@@ -127,9 +130,9 @@ def tile_moe_hot_s_glu_sigmoid_kernel(
             gather_into(t[:], into, window, first, end)
 
         xw_words = xw[:].bitcast(U32)
-        bytes_early = held.tile([P, PASSES, 2 * C], U8, name="bytes_early", align_bytes=64)
+        bytes_early = held.tile([P, PASSES, 3 * C], U8, name="bytes_early", align_bytes=64)
         words_early = held.tile([P, PASSES, (E - LATE_SLOTS) * C], U32, name="words_early", align_bytes=64)
-        gather_into(bytes_early[:], slot_bytes, xs, E - 2, E)
+        gather_into(bytes_early[:], slot_bytes, xs, E - 3, E)
         gather_into(words_early[:, :, (E - LATE_SLOTS - 1) * C :], slot_words, xw_words, E - 1, E)
         gather_into(words_early[:, :, : (E - LATE_SLOTS - 1) * C], slot_words, xw_words, LATE_SLOTS, E - 1)
 
@@ -155,9 +158,11 @@ def tile_moe_hot_s_glu_sigmoid_kernel(
         HALF = H // 2
 
         def result_in(e):
-            if e >= 2:
-                return result_banks[0][:, (e - 2) * C : (e - 1) * C]
-            return (result_banks[1] if e else gate_banks[1])[:, :C]
+            if e >= 4:
+                return result_banks[0][:, (e - 4) * C : (e - 3) * C]
+            if e:
+                return result_banks[1][:, (e - 1) * C : e * C]
+            return gate_banks[1][:, :C]
 
         def halved(tiles, u):
             return [t[:, u * HALF : (u + 1) * HALF] for t in tiles]
@@ -233,8 +238,8 @@ def tile_moe_hot_s_glu_sigmoid_kernel(
             gate = gates(i)
             if not e:
                 quantised[ORDER[i - 1]] = quantise(i - 1)
-            if i < 2:
-                gather(slot_bytes, xs, U8, "w1_%d" % e, 2 - 2 * i, 4 - 2 * i)
+            if i == 0:
+                gather(slot_bytes, xs, U8, "w1_%d" % e, 0, E - 3)
             if e:
                 products(e, w3[e], s3[e], lin_sums(i))
             else:
@@ -243,18 +248,18 @@ def tile_moe_hot_s_glu_sigmoid_kernel(
             for j in behind:
                 turn(j, hs[j])
             hs[i] = hidden(i, gate)
-            if i in (1, 2):
-                gather(slot_words, xw_words, U32, "w3_%d" % e, 2 - i, 3 - i)
+            if i == 1:
+                gather(slot_words, xw_words, U32, "w3_%d" % e, 0, LATE_SLOTS)
             for j in behind:
                 quantised[ORDER[j]] = quantise(j)
         turn(E - 1, hs[E - 1])
         quantised[0] = quantise(E - 1)
         for e in range(COLD, 0, -1):
             second_layer(e, *quantised[e])
-        nc.scalar.copy(ysb[:, 2 * C :], result_banks[0][:])
-        nc.sync.dma_start(out[:, 2 * C :], ysb[:, 2 * C :])
+        nc.scalar.copy(ysb[:, 4 * C :], result_banks[0][:, : 2 * C])
+        nc.sync.dma_start(out[:, 4 * C :], ysb[:, 4 * C :])
         second_layer(0, *quantised[0])
-        nc.vector.tensor_copy(ysb[:, C : 2 * C], result_in(1))
-        nc.sync.dma_start(out[:, C : 2 * C], ysb[:, C : 2 * C])
+        nc.vector.tensor_copy(ysb[:, C : 4 * C], result_banks[1][:, : 3 * C])
+        nc.sync.dma_start(out[:, C : 4 * C], ysb[:, C : 4 * C])
         nc.scalar.copy(ysb[:, :C], result_in(0))
         nc.sync.dma_start(out[:, :C], ysb[:, :C])

@@ -35,21 +35,21 @@ def tile_moe_hot_s_glu_sigmoid_kernel(
         ring = ctx.enter_context(tc.tile_pool(name="ring", bufs=3))
         psum = ctx.enter_context(tc.psum_pool(name="psum", bufs=1))
 
-        def load_rows(plane, scales, queue, rows):
+        def load_rows(plane, scales, rows):
             by_row = scales.bitcast(I32).rearrange("f s (q r) n -> r q (f s) n", r=4)
             for r in rows:
-                queue.dma_start(plane[:].bitcast(I32)[r:P:32, :, :], by_row[r])
+                nc.sync.dma_start(plane[:].bitcast(I32)[r:P:32, :, :], by_row[r])
 
-        def load_plane(name, scales, queue, rows=range(4)):
+        def load_plane(name, scales, rows=range(4)):
             count, passes, blocks, width = scales.shape
             plane = held.tile([P, count * passes, width], U8, name=name, align_bytes=64)
-            load_rows(plane, scales, queue, rows)
+            load_rows(plane, scales, rows)
             return plane
 
         w1, w3, w2, s1, s3 = {}, {}, {}, {}, {}
 
-        def load_cold_rows(into, name, scales, first, end, queue):
-            plane = load_plane(name, scales[first - 1 : end - 1], queue)
+        def load_cold_rows(into, name, scales, first, end):
+            plane = load_plane(name, scales[first - 1 : end - 1])
             for e in range(first, end):
                 into[e] = [plane[:, (e - first) * PASSES + s, :] for s in range(PASSES)]
 
@@ -72,23 +72,20 @@ def tile_moe_hot_s_glu_sigmoid_kernel(
         for r in range(4):
             nc.sync.dma_start(xs[:].bitcast(I32)[r:P:32, :, :], token_rows[r])
         nc.sync.dma_start(xw[:], x_words.rearrange("s p t d -> p s (t d)").bitcast(I32))
-        load_cold_rows(s1, "s1c_early", w1c_scales, LATE_ROWS, E, nc.sync)
+        load_cold_rows(s1, "s1c_early", w1c_scales, LATE_ROWS, E)
+        load_cold_rows(s3, "s3c_early", w3c_scales, LATE_ROWS, E)
+        s2h = load_plane("s2h", w2h_scales, range(2))
         load_cold_words(w3, "w3", w3c_words, ORDER[0])
-        load_cold_rows(s3, "s3c_early", w3c_scales, LATE_ROWS, E, nc.sync)
-        s2h = held.tile([P, 1, N], U8, name="s2h", align_bytes=64)
-        for i, e in enumerate(ORDER[1:COLD]):
+        for e in ORDER[1:COLD]:
+            if e == LATE_ROWS - 1:
+                load_cold_rows(s1, "s1c_late", w1c_scales, 1, LATE_ROWS)
+                load_cold_rows(s3, "s3c_late", w3c_scales, 1, LATE_ROWS)
             load_cold_words(w1, "w1", w1c_words, e)
-            if i < 3:
-                load_rows(s2h, w2h_scales, nc.sync, [i])
             load_cold_words(w3, "w3", w3c_words, e)
-            if i == 0:
-                load_cold_rows(s1, "s1c_late", w1c_scales, 1, LATE_ROWS, nc.sync)
-            if i == 1:
-                load_cold_rows(s3, "s3c_late", w3c_scales, 1, LATE_ROWS, nc.sync)
-            if i == 2:
-                s1h = load_plane("s1h", w1h_scales, nc.sync)
-            if i == 3:
-                s3h = load_plane("s3h", w3h_scales, nc.sync)
+            if e == 2:
+                s1h = load_plane("s1h", w1h_scales)
+            if e == 1:
+                s3h = load_plane("s3h", w3h_scales)
         w1[0] = []
         for first, end in ((0, PASSES - 1), (PASSES - 1, PASSES)):
             t = held.tile([P, end - first, 4 * H], U8, name="w1h_%d" % first, align_bytes=64)
@@ -106,10 +103,10 @@ def tile_moe_hot_s_glu_sigmoid_kernel(
                     hot3[(s, u)] = t[:, (u - first) * 2 * H : (u - first + 1) * 2 * H].bitcast(FP8X4)
         w2c = held.tile([P, COLD, 2 * N], U8, name="w2c", align_bytes=64)
         nc.sync.dma_start(w2c[:].bitcast(I32), w2c_words.bitcast(I32).rearrange("f s p n -> p (f s) n"))
-        s2c = load_plane("s2c", w2c_scales, nc.sync)
+        s2c = load_plane("s2c", w2c_scales)
         w2h = held.tile([P, 4 * N], U8, name="w2h", align_bytes=64)
         nc.sync.dma_start(w2h[:].bitcast(I32), w2h_words[0, 0].rearrange("p n d -> p (n d)").bitcast(I32))
-        load_rows(s2h, w2h_scales, nc.sync, [3])
+        load_rows(s2h, w2h_scales, range(2, 4))
         for e in range(1, E):
             w2[e] = (w2c[:, e - 1, :].bitcast(FP4X4), s2c[:, e - 1, :])
         w2[0] = (w2h[:].bitcast(FP8X4), s2h[:, 0, :])

@@ -48,10 +48,11 @@ def tile_moe_hot_s_glu_sigmoid_kernel(
 
         w1, w3, w2, s1, s3 = {}, {}, {}, {}, {}
 
-        def load_cold_rows(into, name, scales, first, end):
-            plane = load_plane(name, scales[first - 1 : end - 1])
+        def load_cold_rows(into, name, scales, first, end, rows=range(4)):
+            plane = load_plane(name, scales[first - 1 : end - 1], rows)
             for e in range(first, end):
                 into[e] = [plane[:, (e - first) * PASSES + s, :] for s in range(PASSES)]
+            return plane
 
         def load_cold_words(into, name, words, e):
             t = held.tile([P, PASSES, 2 * H], U8, name="%s_%d" % (name, e), align_bytes=64)
@@ -71,10 +72,11 @@ def tile_moe_hot_s_glu_sigmoid_kernel(
         token_rows = x_scales.bitcast(I32).rearrange("s (q r) n -> r q s n", r=4)
         for r in range(4):
             nc.sync.dma_start(xs[:].bitcast(I32)[r:P:32, :, :], token_rows[r])
+        s1_early = load_cold_rows(s1, "s1c_early", w1c_scales, LATE_ROWS, E, range(2))
         nc.sync.dma_start(xw[:], x_words.rearrange("s p t d -> p s (t d)").bitcast(I32))
-        load_cold_rows(s1, "s1c_early", w1c_scales, LATE_ROWS, E)
+        load_rows(s1_early, w1c_scales[LATE_ROWS - 1 :], range(2, 4))
         load_cold_rows(s3, "s3c_early", w3c_scales, LATE_ROWS, E)
-        s2h = load_plane("s2h", w2h_scales, range(2))
+        s1h = load_plane("s1h", w1h_scales)
         load_cold_words(w3, "w3", w3c_words, ORDER[0])
         for e in ORDER[1:COLD]:
             if e == LATE_ROWS - 1:
@@ -82,10 +84,7 @@ def tile_moe_hot_s_glu_sigmoid_kernel(
                 load_cold_rows(s3, "s3c_late", w3c_scales, 1, LATE_ROWS)
             load_cold_words(w1, "w1", w1c_words, e)
             load_cold_words(w3, "w3", w3c_words, e)
-            if e == 2:
-                s1h = load_plane("s1h", w1h_scales)
-            if e == 1:
-                s3h = load_plane("s3h", w3h_scales)
+        s3h = load_plane("s3h", w3h_scales)
         w1[0] = []
         for first, end in ((0, PASSES - 1), (PASSES - 1, PASSES)):
             t = held.tile([P, end - first, 4 * H], U8, name="w1h_%d" % first, align_bytes=64)
@@ -106,7 +105,7 @@ def tile_moe_hot_s_glu_sigmoid_kernel(
         s2c = load_plane("s2c", w2c_scales)
         w2h = held.tile([P, 4 * N], U8, name="w2h", align_bytes=64)
         nc.sync.dma_start(w2h[:].bitcast(I32), w2h_words[0, 0].rearrange("p n d -> p (n d)").bitcast(I32))
-        load_rows(s2h, w2h_scales, range(2, 4))
+        s2h = load_plane("s2h", w2h_scales)
         for e in range(1, E):
             w2[e] = (w2c[:, e - 1, :].bitcast(FP4X4), s2c[:, e - 1, :])
         w2[0] = (w2h[:].bitcast(FP8X4), s2h[:, 0, :])
@@ -170,9 +169,11 @@ def tile_moe_hot_s_glu_sigmoid_kernel(
             return [gate_banks[(i + u) % 2][:, :HALF] for u in range(2)]
 
         def lin_sums(i):
-            if i < 2:
-                return [lin_banks[1][i][:]]
-            return [lin_banks[i % 2][u][:, :HALF] for u in range(2)]
+            if i in (0, 1, 3):
+                return [lin_banks[1][i % 3][:]]
+            if i == E - 1:
+                return [lin_banks[1][1 - u][:, :HALF] for u in range(2)]
+            return [lin_banks[0][u][:, :HALF] for u in range(2)]
 
         def products(e, words, scales, sums):
             if len(sums) == 1:
@@ -197,7 +198,7 @@ def tile_moe_hot_s_glu_sigmoid_kernel(
             return h
 
         def turned_in(i):
-            banks = [lin_banks[0][0], lin_banks[0][1], lin_banks[1][1], lin_banks[0][1], gate_banks[0], lin_banks[0][0]]
+            banks = [lin_banks[0][0], lin_banks[0][1], lin_banks[0][0], lin_banks[0][1], gate_banks[0], lin_banks[0][0]]
             return banks[i][:, HALF:]
 
         def turn(i, h):
@@ -241,7 +242,7 @@ def tile_moe_hot_s_glu_sigmoid_kernel(
                 products(e, w3[e], s3[e], lin_sums(i))
             else:
                 first_layer(e, [([hot3[(s, u)] for s in range(PASSES)], halved(s3[e], u), lin_sums(i)[u]) for u in range(2)])
-            behind = {2: [0, 1], 3: [2], 4: [3]}.get(i, [])
+            behind = {2: [0, 1], 4: [2, 3]}.get(i, [])
             for j in behind:
                 turn(j, hs[j])
             hs[i] = hidden(i, gate)

@@ -76,7 +76,7 @@ def tile_moe_hot_s_glu_sigmoid_kernel(
         nc.sync.dma_start(xw[:], x_words.rearrange("s p t d -> p s (t d)").bitcast(I32))
         load_rows(s1_early, w1c_scales[LATE_ROWS - 1 :], range(2, 4))
         load_cold_rows(s3, "s3c_early", w3c_scales, LATE_ROWS, E)
-        s1h = load_plane("s1h", w1h_scales)
+        s1h = load_plane("s1h", w1h_scales, range(2))
         load_cold_words(w3, "w3", w3c_words, ORDER[0])
         for e in ORDER[1:COLD]:
             if e == LATE_ROWS - 1:
@@ -84,6 +84,8 @@ def tile_moe_hot_s_glu_sigmoid_kernel(
                 load_cold_rows(s3, "s3c_late", w3c_scales, 1, LATE_ROWS)
             load_cold_words(w1, "w1", w1c_words, e)
             load_cold_words(w3, "w3", w3c_words, e)
+            if e == 2:
+                load_rows(s1h, w1h_scales, range(2, 4))
         s3h = load_plane("s3h", w3h_scales)
         w1[0] = []
         for first, end in ((0, PASSES - 1), (PASSES - 1, PASSES)):
@@ -169,11 +171,9 @@ def tile_moe_hot_s_glu_sigmoid_kernel(
             return [gate_banks[(i + u) % 2][:, :HALF] for u in range(2)]
 
         def lin_sums(i):
-            if i in (0, 1, 3):
-                return [lin_banks[1][i % 3][:]]
-            if i == E - 1:
-                return [lin_banks[1][1 - u][:, :HALF] for u in range(2)]
-            return [lin_banks[0][u][:, :HALF] for u in range(2)]
+            if i < 2:
+                return [lin_banks[1][i][:]]
+            return [lin_banks[i % 2][u][:, :HALF] for u in range(2)]
 
         def products(e, words, scales, sums):
             if len(sums) == 1:
@@ -198,7 +198,7 @@ def tile_moe_hot_s_glu_sigmoid_kernel(
             return h
 
         def turned_in(i):
-            banks = [lin_banks[0][0], lin_banks[0][1], lin_banks[0][0], lin_banks[0][1], gate_banks[0], lin_banks[0][0]]
+            banks = [lin_banks[0][0], lin_banks[0][1], lin_banks[1][1], lin_banks[0][1], gate_banks[0], lin_banks[0][0]]
             return banks[i][:, HALF:]
 
         def turn(i, h):
@@ -242,7 +242,7 @@ def tile_moe_hot_s_glu_sigmoid_kernel(
                 products(e, w3[e], s3[e], lin_sums(i))
             else:
                 first_layer(e, [([hot3[(s, u)] for s in range(PASSES)], halved(s3[e], u), lin_sums(i)[u]) for u in range(2)])
-            behind = {2: [0, 1], 4: [2, 3]}.get(i, [])
+            behind = {2: [0, 1], 3: [2], 4: [3]}.get(i, [])
             for j in behind:
                 turn(j, hs[j])
             hs[i] = hidden(i, gate)

from contextlib import ExitStack

import concourse.mybir as mybir
from concourse.masks import make_identity

K, T, E, C, H, N = 1536, 768, 6, 128, 512, 128
P = 128
PASSES = K // 512
COLD = E - 1
FLOPS = 2 * E * C * (2 * K * H + H * N)

F32 = mybir.dt.float32
BF16 = mybir.dt.bfloat16
I32 = mybir.dt.int32
U32 = mybir.dt.uint32
U16 = mybir.dt.uint16
U8 = mybir.dt.uint8
FP8X4 = mybir.dt.float8_e4m3fn_x4
FP4X4 = mybir.dt.float4_e2m1fn_x4
SIGMOID = mybir.ActivationFunctionType.Sigmoid
MULT = mybir.AluOpType.mult

ORDER = list(range(E - 1, -1, -1))
LATE_SLOTS = 2
LATE_ROWS = 3


def tile_moe_hot_s_glu_sigmoid_kernel(
    tc, x_words, x_scales, w1h_words, w1h_scales, w3h_words, w3h_scales, w2h_words, w2h_scales,
    w1c_words, w1c_scales, w3c_words, w3c_scales, w2c_words, w2c_scales, offs, out,
):
    nc = tc.nc
    with ExitStack() as ctx:
        held = ctx.enter_context(tc.tile_pool(name="held", bufs=1))
        ring = ctx.enter_context(tc.tile_pool(name="ring", bufs=3))
        psum = ctx.enter_context(tc.psum_pool(name="psum", bufs=1))

        def load_rows(plane, scales, rows):
            by_row = scales.bitcast(I32).rearrange("f s (q r) n -> r q (f s) n", r=4)
            for r in rows:
                nc.sync.dma_start(plane[:].bitcast(I32)[r:P:32, :, :], by_row[r])

        def load_plane(name, scales, rows=range(4)):
            count, passes, blocks, width = scales.shape
            plane = held.tile([P, count * passes, width], U8, name=name, align_bytes=64)
            load_rows(plane, scales, rows)
            return plane

        w1, w3, w2, s1, s3 = {}, {}, {}, {}, {}

        def load_cold_rows(into, name, scales, first, end, rows=range(4)):
            plane = load_plane(name, scales[first - 1 : end - 1], rows)
            for e in range(first, end):
                into[e] = [plane[:, (e - first) * PASSES + s, :] for s in range(PASSES)]
            return plane

        def load_cold_words(into, name, words, e):
            t = held.tile([P, PASSES, 2 * H], U8, name="%s_%d" % (name, e), align_bytes=64)
            nc.sync.dma_start(t[:].bitcast(I32), words[e - 1].bitcast(I32).rearrange("s p n -> p s n"))
            into[e] = [t[:, s, :].bitcast(FP4X4) for s in range(PASSES)]


        offsets = held.tile([P, E * C // 16], U16, name="offsets")
        xs = held.tile([P, PASSES, T], U8, name="xs", align_bytes=64)
        nc.vector.memset(xs[:].rearrange("p a n -> p (a n)").bitcast(I32), 0)
        xw = held.tile([P, PASSES, T], I32, name="xw", align_bytes=64)
        ident = held.tile([P, P], F32, name="ident")
        make_identity(nc, ident[:])

        load_cold_words(w1, "w1", w1c_words, ORDER[0])
        nc.sync.dma_start(offsets[:], offs)
        token_rows = x_scales.bitcast(I32).rearrange("s (q r) n -> r q s n", r=4)
        for r in range(4):
            nc.sync.dma_start(xs[:].bitcast(I32)[r:P:32, :, :], token_rows[r])
        s1_early = load_cold_rows(s1, "s1c_early", w1c_scales, LATE_ROWS, E, range(2))
        nc.sync.dma_start(xw[:], x_words.rearrange("s p t d -> p s (t d)").bitcast(I32))
        load_rows(s1_early, w1c_scales[LATE_ROWS - 1 :], range(2, 4))
        load_cold_rows(s3, "s3c_early", w3c_scales, LATE_ROWS, E)
        s1h = load_plane("s1h", w1h_scales, range(2))
        load_cold_words(w3, "w3", w3c_words, ORDER[0])
        for e in ORDER[1:COLD]:
            if e == LATE_ROWS - 1:
                load_cold_rows(s1, "s1c_late", w1c_scales, 1, LATE_ROWS)
                load_cold_rows(s3, "s3c_late", w3c_scales, 1, LATE_ROWS)
            load_cold_words(w1, "w1", w1c_words, e)
            load_cold_words(w3, "w3", w3c_words, e)
            if e == 2:
                load_rows(s1h, w1h_scales, range(2, 4))
        s3h = load_plane("s3h", w3h_scales)
        w1[0] = []
        for first, end in ((0, PASSES - 1), (PASSES - 1, PASSES)):
            t = held.tile([P, end - first, 4 * H], U8, name="w1h_%d" % first, align_bytes=64)
            nc.sync.dma_start(t[:].bitcast(I32), w1h_words[0, first:end].rearrange("s p n d -> p s (n d)").bitcast(I32))
            w1[0].extend(t[:, s, :].bitcast(FP8X4) for s in range(end - first))
        s1[0] = [s1h[:, s, :] for s in range(PASSES)]
        s3[0] = [s3h[:, s, :] for s in range(PASSES)]
        hot3 = {}
        for s in range(PASSES):
            src = w3h_words[0, s].rearrange("p n d -> p (n d)").bitcast(I32)
            for first, end in [(0, 2)] if s < PASSES - 1 else [(0, 1), (1, 2)]:
                t = held.tile([P, (end - first) * 2 * H], U8, name="w3h_%d_%d" % (s, first), align_bytes=64)
                nc.sync.dma_start(t[:].bitcast(I32), src[:, first * H // 2 : end * H // 2])
                for u in range(first, end):
                    hot3[(s, u)] = t[:, (u - first) * 2 * H : (u - first + 1) * 2 * H].bitcast(FP8X4)
        w2c = held.tile([P, COLD, 2 * N], U8, name="w2c", align_bytes=64)
        nc.sync.dma_start(w2c[:].bitcast(I32), w2c_words.bitcast(I32).rearrange("f s p n -> p (f s) n"))
        s2c = load_plane("s2c", w2c_scales)
        w2h = held.tile([P, 4 * N], U8, name="w2h", align_bytes=64)
        nc.sync.dma_start(w2h[:].bitcast(I32), w2h_words[0, 0].rearrange("p n d -> p (n d)").bitcast(I32))
        s2h = load_plane("s2h", w2h_scales)
        for e in range(1, E):
            w2[e] = (w2c[:, e - 1, :].bitcast(FP4X4), s2c[:, e - 1, :])
        w2[0] = (w2h[:].bitcast(FP8X4), s2h[:, 0, :])

        ysb = held.tile([P, E * C], F32, name="ysb")

        slot_words, slot_bytes = {}, {}

        def gather_into(t, into, window, first, end):
            entries = offsets[:, first * C // 16 : end * C // 16]
            for s in range(PASSES):
                nc.vector.tensor_copy(t[:, s, :], window[:, s, :].indirect(entries))
            for e in range(first, end):
                into[e] = [t[:, s, (e - first) * C : (e - first + 1) * C] for s in range(PASSES)]

        def gather(into, window, dtype, name, first, end):
            t = held.tile([P, PASSES, (end - first) * C], dtype, name=name, align_bytes=64)
            gather_into(t[:], into, window, first, end)

        xw_words = xw[:].bitcast(U32)
        bytes_early = held.tile([P, PASSES, 3 * C], U8, name="bytes_early", align_bytes=64)
        words_early = held.tile([P, PASSES, (E - LATE_SLOTS) * C], U32, name="words_early", align_bytes=64)
        gather_into(bytes_early[:], slot_bytes, xs, E - 3, E)
        gather_into(words_early[:, :, (E - LATE_SLOTS - 1) * C :], slot_words, xw_words, E - 1, E)
        gather_into(words_early[:, :, : (E - LATE_SLOTS - 1) * C], slot_words, xw_words, LATE_SLOTS, E - 1)

        def first_layer(e, parts):
            for s in range(PASSES):
                for words, scales, acc in parts:
                    nc.tensor.matmul_mx(
                        out=acc,
                        lhsT=slot_words[e][s].bitcast(FP8X4),
                        lhsT_scale=slot_bytes[e][s],
                        rhs=words[s],
                        rhs_scale=scales[s],
                        start=(s == 0),
                        stop=(s == PASSES - 1),
                    )

        def paired(acc):
            return acc.rearrange("j (p u v) -> j u p v", u=2, v=2)

        gate_banks = [psum.tile([P, H], F32, name="gate_bank%d" % j) for j in range(2)]
        lin_banks = [[psum.tile([P, H], F32, name="lin_bank%d_%d" % (j, u)) for u in range(2)] for j in range(2)]
        result_banks = [psum.tile([P, H], F32, name="result_bank%d" % j) for j in range(2)]
        HALF = H // 2

        def result_in(e):
            if e >= 4:
                return result_banks[0][:, (e - 4) * C : (e - 3) * C]
            if e:
                return result_banks[1][:, (e - 1) * C : e * C]
            return gate_banks[1][:, :C]

        def halved(tiles, u):
            return [t[:, u * HALF : (u + 1) * HALF] for t in tiles]

        def gate_sums(i):
            if ORDER[i]:
                return [gate_banks[i % 2][:]]
            return [gate_banks[(i + u) % 2][:, :HALF] for u in range(2)]

        def lin_sums(i):
            if i < 2:
                return [lin_banks[1][i][:]]
            return [lin_banks[i % 2][u][:, :HALF] for u in range(2)]

        def products(e, words, scales, sums):
            if len(sums) == 1:
                first_layer(e, [(words, scales, sums[0])])
            else:
                first_layer(e, [(halved(words, u), halved(scales, u), sums[u]) for u in range(2)])

        def rows_of(sums, u):
            return slice(u * P // len(sums), (u + 1) * P // len(sums))

        def gates(i):
            gate = ring.tile([P, 2, P, 2], F32, name="gate")
            for u, acc in enumerate(gate_sums(i)):
                nc.scalar.activation(gate[:, :, rows_of(gate_sums(i), u), :], paired(acc), SIGMOID)
            return gate

        def hidden(i, gate):
            h = ring.tile([P, 2, P, 2], BF16, name="h", align_bytes=64)
            for u, acc in enumerate(lin_sums(i)):
                rows = rows_of(lin_sums(i), u)
                nc.vector.tensor_tensor(h[:, :, rows, :], paired(acc), gate[:, :, rows, :], MULT)
            return h

        def turned_in(i):
            banks = [lin_banks[0][0], lin_banks[0][1], lin_banks[1][1], lin_banks[0][1], gate_banks[0], lin_banks[0][0]]
            return banks[i][:, HALF:]

        def turn(i, h):
            pairs = h[:].rearrange("j u p v -> j (u p v)").bitcast(F32)
            for u in range(2):
                nc.tensor.transpose(turned_in(i)[:, u * C : (u + 1) * C], pairs[:, u * P : (u + 1) * P], ident[:])

        def quantise(i):
            ht = ring.tile([P, 4 * C], BF16, name="ht", align_bytes=64)
            nc.scalar.copy(
                ht[:].bitcast(F32).rearrange("p (j u) -> p j u", u=2),
                turned_in(i).rearrange("p (u j) -> p j u", u=2),
            )
            codes = held.tile([P, C], U32, name="codes%d" % i, align_bytes=64)
            scales = held.tile([P, C], U8, name="scales%d" % i, align_bytes=64)
            nc.vector.quantize_mx(out=codes[:].bitcast(FP8X4), scales=scales[:], in_=ht[:])
            return codes, scales

        def second_layer(e, codes, scales):
            nc.tensor.matmul_mx(
                out=result_in(e),
                lhsT=w2[e][0],
                lhsT_scale=w2[e][1],
                rhs=codes[:].bitcast(FP8X4),
                rhs_scale=scales[:],
                start=True,
                stop=True,
            )

        hs, quantised = {}, {}
        for i, e in enumerate(ORDER):
            products(e, w1[e], s1[e], gate_sums(i))
            if not e:
                turn(i - 1, hs[i - 1])
            gate = gates(i)
            if not e:
                quantised[ORDER[i - 1]] = quantise(i - 1)
            if i == 0:
                gather(slot_bytes, xs, U8, "w1_%d" % e, 0, E - 3)
            if e:
                products(e, w3[e], s3[e], lin_sums(i))
            else:
                first_layer(e, [([hot3[(s, u)] for s in range(PASSES)], halved(s3[e], u), lin_sums(i)[u]) for u in range(2)])
            behind = {2: [0, 1], 3: [2], 4: [3]}.get(i, [])
            for j in behind:
                turn(j, hs[j])
            hs[i] = hidden(i, gate)
            if i == 1:
                gather(slot_words, xw_words, U32, "w3_%d" % e, 0, LATE_SLOTS)
            for j in behind:
                quantised[ORDER[j]] = quantise(j)
        turn(E - 1, hs[E - 1])
        quantised[0] = quantise(E - 1)
        for e in range(COLD, 0, -1):
            second_layer(e, *quantised[e])
        nc.scalar.copy(ysb[:, 4 * C :], result_banks[0][:, : 2 * C])
        nc.sync.dma_start(out[:, 4 * C :], ysb[:, 4 * C :])
        second_layer(0, *quantised[0])
        nc.vector.tensor_copy(ysb[:, C : 4 * C], result_banks[1][:, : 3 * C])
        nc.sync.dma_start(out[:, C : 4 * C], ysb[:, C : 4 * C])
        nc.scalar.copy(ysb[:, :C], result_in(0))
        nc.sync.dma_start(out[:, :C], ysb[:, :C])
